import numpy as np
import ml_dtypes


def mxq(x, axis, fmt="e4m3"):
    dtype, down = {"e4m3": (ml_dtypes.float8_e4m3fn, 7), "e5m2": (ml_dtypes.float8_e5m2, 14)}[fmt]
    v = np.moveaxis(np.asarray(x, np.float32).astype(ml_dtypes.bfloat16).astype(np.float64), axis, -1)
    blocks = v.reshape(v.shape[:-1] + (-1, 32))
    amax = np.abs(blocks).max(-1, keepdims=True)
    byte = np.maximum(np.where(amax > 0, np.frexp(amax)[1] - 1 + 127, 0) - down, 1)
    scale = np.exp2(byte - 127.0)
    codes = (blocks / scale).astype(np.float32).astype(dtype).astype(np.float64)
    return np.moveaxis((codes * scale).reshape(v.shape), -1, axis)


WIDE = False


def mx_kscale(k):
    if not WIDE:
        return np.ones(k)
    levels = np.array([10, -10, 5, -5, 0])
    if k % 512:
        return np.exp2(np.random.permutation(np.resize(levels, k // 32))).repeat(32)
    a = np.empty((k // 512, 16))
    for p in range(k // 512):
        a[p, :8] = np.random.permutation(np.resize(levels, 8))
        for g in range(8):
            far = levels[np.abs(levels - a[p, g]) >= 10]
            a[p, g + 8] = far[np.random.randint(len(far))]
    return np.exp2(a.ravel()).repeat(32)


def f64(x):
    return np.asarray(x).astype(np.float64)


def striped(idx):
    return np.tile(np.asarray(idx).reshape(-1, 16).T, (8, 1)).astype(np.uint16)


def unstriped(offs):
    return offs[:16].T.reshape(-1).astype(np.int64)


E2M1 = np.array([0.0, 0.5, 1.0, 1.5, 2.0, 3.0, 4.0, 6.0, -0.0, -0.5, -1.0, -1.5, -2.0, -3.0, -4.0, -6.0])


def pack_weight(w, fmt):
    k, n = w.shape
    w = f64(np.asarray(w, np.float32).astype(ml_dtypes.bfloat16)).reshape(k // 32, 32, n)
    amax = np.abs(w).max(1)
    if fmt == "e4m3":
        byte = np.frexp(amax)[1] - 1 + 127 - 7
    else:
        mant, ex = np.frexp(amax / 6.0)
        byte = np.where(mant > 0.5, ex, ex - 1) + 127
    byte = np.clip(np.where(amax > 0, byte, 1), 1, 254)
    scaled = (w * np.exp2(127.0 - byte)[:, None, :]).reshape(k, n).astype(np.float32)
    by_word = np.ascontiguousarray(scaled.reshape(k // 512, 128, 4, n).transpose(0, 1, 3, 2))
    if fmt == "e4m3":
        words = by_word.astype(ml_dtypes.float8_e4m3fn).view(np.uint8)
    else:
        c = by_word.astype(ml_dtypes.float4_e2m1fn).view(np.uint8) & 0xF
        words = (c[..., 0::2] | (c[..., 1::2] << 4)).reshape(k // 512, 128, 2 * n)
    return np.ascontiguousarray(words), np.ascontiguousarray(byte.astype(np.uint8).reshape(k // 512, 16, n))


def unpack_weight(words, scales, fmt):
    g, _, n = scales.shape
    words = np.ascontiguousarray(words).reshape(g, 128, n, -1)
    if fmt == "e4m3":
        vals = words.view(ml_dtypes.float8_e4m3fn).astype(np.float64)
    else:
        nib = np.empty((g, 128, n, 4), np.uint8)
        nib[..., 0::2] = words & 0xF
        nib[..., 1::2] = words >> 4
        vals = E2M1[nib]
    vals = vals * np.repeat(np.exp2(scales.astype(np.float64) - 127.0), 8, axis=1)[..., None]
    return vals.transpose(0, 1, 3, 2).reshape(g * 512, n)


B, N, T, D, NQ = 1, 512, 2048, 1024, 128


def setup_inputs():
    n = np.random.standard_normal
    idx = np.random.permutation(T)[:B * N]
    s = mx_kscale(D)[:, None]
    kp = pack_weight(n((D, T)) / s, "e2m1")
    cp = pack_weight(n((D, T)) / s, "e2m1")
    return {
        "qT": (n((B, D, NQ)) * s * (1.00 / np.sqrt(D))).astype(np.float32),
        "k_words": np.ascontiguousarray(kp[0].reshape(1, 2, 128, T, 2).transpose(0, 2, 3, 1, 4)).reshape(1, 128, T, 4),
        "k_scales": kp[1],
        "c_words": np.ascontiguousarray(cp[0].reshape(1, 2, 128, T, 2).transpose(0, 2, 3, 1, 4)).reshape(1, 128, T, 4),
        "c_scales": cp[1],
        "nb": np.tile(0.5 * n(2048), (128, 1)).astype(np.float32),
        "offs": striped(idx),
    }


def reference(qT, k_words, k_scales, c_words, c_scales, nb, offs):
    idx = unstriped(offs)
    pick = lambda x, which: x[:, which].reshape(x.shape[0], B, -1).transpose(1, 0, 2)
    k = unpack_weight(k_words.reshape(1, 128, T, 2, 2).transpose(0, 3, 1, 2, 4).reshape(2, 128, 2 * T), k_scales, "e2m1")
    kg = pick(k, idx)
    c = unpack_weight(c_words.reshape(1, 128, T, 2, 2).transpose(0, 3, 1, 2, 4).reshape(2, 128, 2 * T), c_scales, "e2m1")
    cg = pick(c, idx)
    qq = mxq(f64(qT), 1, "e4m3")
    a = qq.transpose(0, 2, 1) @ kg
    z = qq.transpose(0, 2, 1) @ cg
    y = np.maximum(a + pick(f64(nb), idx)[:, :1, :], 0.0) * z
    return y

@@ -1,0 +1,151 @@
+from contextlib import ExitStack
+
+import concourse.mybir as mybir
+from concourse.masks import make_identity
+
+NQ, D, T, N = 128, 1024, 2048, 512
+FLOPS = 2 * 2 * NQ * D * N
+
+F32 = mybir.dt.float32
+BF16 = mybir.dt.bfloat16
+I32 = mybir.dt.int32
+U32 = mybir.dt.uint32
+U16 = mybir.dt.uint16
+U8 = mybir.dt.uint8
+FP8X4 = mybir.dt.float8_e4m3fn_x4
+FP4X4 = mybir.dt.float4_e2m1fn_x4
+ACT = mybir.ActivationFunctionType
+ALU = mybir.AluOpType
+
+P = 128
+PACK = 4
+PASSES = D // (P * PACK)
+HALF = P // 2
+QUAD = 32
+ROW0 = 32
+BANK = 512
+PARTS = 2
+PART = N // PARTS
+
+
+def tile_attend_neu_reglu_topk_kernel(tc, qT, k_words, k_scales, c_words, c_scales, nb, offs, out):
+    nc = tc.nc
+    with ExitStack() as ctx:
+        sb = ctx.enter_context(tc.tile_pool(name="sb", bufs=1))
+        ps = ctx.enter_context(tc.psum_pool(name="ps", bufs=1))
+
+        offsets = sb.tile([P, N // 16], U16, name="offsets")
+        nc.sync.dma_start(offsets[:], offs)
+
+        banks, per_bank = T // BANK, BANK // P
+        nb_cols = sb.tile([P, banks, per_bank], F32, name="nb_cols", tag="nb_then_q", align_bytes=64)
+        nc.sync.dma_start(nb_cols[:], nb[0].rearrange("(b n j) -> n b j", b=banks, j=per_bank))
+
+        scale_win = []
+        for name, src in (("k", k_scales), ("c", c_scales)):
+            win = sb.tile([P, T // 4], I32, name=name + "_scale_win", tag=name + "_first", align_bytes=64)
+            nc.vector.memset(win[:], 0)
+            rows = src.bitcast(I32).rearrange("o (h e r) t -> e (o h) r t", h=2, e=2)
+            for e in range(2):
+                first = ROW0 + QUAD * e
+                nc.sync.dma_start(win[first : first + 16, :], rows[e])
+            scale_win.append(win)
+
+        k_win = sb.tile([P, T], I32, name="k_win", align_bytes=64)
+        nc.sync.dma_start(k_win[:], k_words[0].rearrange("p t b -> p (t b)").bitcast(I32))
+        q_raw = sb.tile([P, PASSES, PACK, NQ], F32, name="q_raw")
+        nc.sync.dma_start(
+            q_raw[:].rearrange("p o j w -> p o (j w)"),
+            qT[0].rearrange("(o p j) w -> p o (j w)", o=PASSES, j=PACK),
+        )
+
+        ident = sb.tile([P, P], F32, name="ident")
+        make_identity(nc, ident[:])
+
+        nb_win = sb.tile([P, T], F32, name="nb_win", tag="nb_then_codes", align_bytes=64)
+        for b in range(banks):
+            spread = ps.tile([P, per_bank, P], F32, name="spread%d" % b)
+            for j in range(per_bank):
+                nc.tensor.transpose(spread[:, j, :], nb_cols[:, b, j : j + 1].to_broadcast([P, P]), ident[:])
+            nc.scalar.activation(
+                nb_win[:, b * BANK : (b + 1) * BANK].rearrange("p (n j) -> p n j", j=per_bank),
+                spread[:].rearrange("p j n -> p n j"),
+                ACT.Copy,
+            )
+
+        picked_scales = sb.tile([P, 2, N], U8, name="picked_scales", align_bytes=64)
+        for i in range(2):
+            nc.vector.tensor_copy(picked_scales[:, i, :], scale_win[i][:].bitcast(U8).indirect(offsets[:]))
+        planes = sb.tile([P, PASSES, 2, N], U8, name="planes", align_bytes=64)
+        for o in range(PASSES):
+            for h in range(2):
+                first = ROW0 + 4 * (2 * o + h)
+                nc.sync.dma_start(
+                    planes[HALF * h : HALF * (h + 1), o].rearrange("p i n -> p (i n)").bitcast(I32),
+                    picked_scales[first : first + HALF].rearrange("p i n -> p (i n)").bitcast(I32),
+                )
+
+        c_win = sb.tile([P, T], I32, name="c_win", tag="c_first", align_bytes=64)
+        nc.sync.dma_start(c_win[:], c_words[0].rearrange("p t b -> p (t b)").bitcast(I32))
+
+        q_bf = sb.tile([P, PASSES, NQ, PACK], BF16, name="q_bf", tag="nb_then_q", align_bytes=64)
+        for o in range(PASSES):
+            nc.scalar.activation(q_bf[:, o], q_raw[:, o].rearrange("p j w -> p w j"), ACT.Copy)
+
+        k_pairs = sb.tile([P, N], U32, name="k_pairs", align_bytes=64)
+        nc.vector.tensor_copy(k_pairs[:], k_win[:].bitcast(U32).indirect(offsets[:]))
+        nb_picked = sb.tile([P, N], F32, name="nb_picked", align_bytes=64)
+        nc.vector.tensor_copy(nb_picked[:], nb_win[:].indirect(offsets[:]))
+        k_split = sb.tile([P, PASSES, 2 * N], U8, name="k_split", align_bytes=64)
+        nc.vector.tensor_copy(k_split[:].bitcast(U16), k_pairs[:].bitcast(U16).rearrange("p (n o) -> p o n", o=PASSES))
+
+        q_codes = sb.tile([P, PASSES * NQ], U32, name="q_codes", tag="nb_then_codes", align_bytes=64)
+        q_scales = sb.tile([P, PASSES * NQ], U8, name="q_scales", align_bytes=64)
+        nc.vector.quantize_mx(
+            out=q_codes[:].bitcast(FP8X4), scales=q_scales[:], in_=q_bf[:].rearrange("p o w j -> p (o w j)")
+        )
+
+        def product(acc, words, scales):
+            for o in range(PASSES):
+                nc.tensor.matmul_mx(
+                    out=acc,
+                    lhsT=q_codes[:, o * NQ : (o + 1) * NQ].bitcast(FP8X4),
+                    lhsT_scale=q_scales[:, o * NQ : (o + 1) * NQ],
+                    rhs=words(o).bitcast(FP4X4),
+                    rhs_scale=scales(o),
+                    start=(o == 0),
+                    stop=(o == PASSES - 1),
+                )
+
+        a = ps.tile([P, N], F32, name="a")
+        product(a[:], lambda o: k_split[:, o, :], lambda o: planes[:, o, 0, :])
+
+        c_pairs = []
+        for s in range(PARTS):
+            pairs = sb.tile([P, PART], U32, name="c_pairs%d" % s, tag=("nb_then_q", "c_pairs")[s], align_bytes=64)
+            cols = slice(s * PART // 16, (s + 1) * PART // 16)
+            nc.vector.tensor_copy(pairs[:], c_win[:].bitcast(U32).indirect(offsets[:, cols]))
+            c_pairs.append(pairs)
+        z = []
+        for s in range(PARTS):
+            split = sb.tile([P, PASSES, 2 * PART], U8, name="c_split%d" % s, align_bytes=64)
+            nc.vector.tensor_copy(
+                split[:].bitcast(U16), c_pairs[s][:].bitcast(U16).rearrange("p (n o) -> p o n", o=PASSES)
+            )
+            acc = ps.tile([P, PART], F32, name="z%d" % s)
+            for c in range(PART // P):
+                first = s * PART + c * P
+                product(
+                    acc[:, c * P : (c + 1) * P],
+                    lambda o: split[:, o, 2 * c * P : 2 * (c + 1) * P],
+                    lambda o: planes[:, o, 1, first : first + P],
+                )
+            z.append(acc)
+
+        gate = sb.tile([P, N], F32, name="gate")
+        nc.vector.tensor_tensor(gate[:], a[:], nb_picked[:], ALU.add)
+        for s in range(PARTS):
+            cols = slice(s * PART, (s + 1) * PART)
+            result = sb.tile([P, PART], F32, name="result%d" % s)
+            nc.vector.scalar_tensor_tensor(result[:], gate[:, cols], 0.0, z[s][:], ALU.max, ALU.mult)
+            nc.sync.dma_start(out[0, :, cols], result[:])

@@ -32,24 +32,15 @@ def tile_attend_neu_reglu_topk_kernel(tc, qT, k_words, k_scales, c_words, c_scal
     nc = tc.nc
     with ExitStack() as ctx:
         sb = ctx.enter_context(tc.tile_pool(name="sb", bufs=1))
+        shared = ctx.enter_context(tc.tile_pool(name="shared", bufs=1))
         ps = ctx.enter_context(tc.psum_pool(name="ps", bufs=1))
 
         offsets = sb.tile([P, N // 16], U16, name="offsets")
         nc.sync.dma_start(offsets[:], offs)
 
         banks, per_bank = T // BANK, BANK // P
-        nb_cols = sb.tile([P, banks, per_bank], F32, name="nb_cols", tag="nb_then_q", align_bytes=64)
+        nb_cols = shared.tile([P, banks, per_bank], F32, name="nb_cols", offset=2 * PASSES * N - 32)
         nc.sync.dma_start(nb_cols[:], nb[0].rearrange("(b n j) -> n b j", b=banks, j=per_bank))
-
-        scale_win = []
-        for name, src in (("k", k_scales), ("c", c_scales)):
-            win = sb.tile([P, T // 4], I32, name=name + "_scale_win", tag=name + "_first", align_bytes=64)
-            nc.vector.memset(win[:], 0)
-            rows = src.bitcast(I32).rearrange("o (h e r) t -> e (o h) r t", h=2, e=2)
-            for e in range(2):
-                first = ROW0 + QUAD * e
-                nc.sync.dma_start(win[first : first + 16, :], rows[e])
-            scale_win.append(win)
 
         k_win = sb.tile([P, T], I32, name="k_win", align_bytes=64)
         nc.sync.dma_start(k_win[:], k_words[0].rearrange("p t b -> p (t b)").bitcast(I32))
@@ -58,11 +49,21 @@ def tile_attend_neu_reglu_topk_kernel(tc, qT, k_words, k_scales, c_words, c_scal
             q_raw[:].rearrange("p o j w -> p o (j w)"),
             qT[0].rearrange("(o p j) w -> p o (j w)", o=PASSES, j=PACK),
         )
+        scale_win = []
+        for name, src in (("k", k_scales), ("c", c_scales)):
+            win = sb.tile([P, T // 4], I32, name=name + "_scale_win", tag=name + "_scale_slot", align_bytes=64)
+            nc.vector.memset(win[:], 0)
+            rows = src.bitcast(I32).rearrange("o (h e r) t -> e (o h) r t", h=2, e=2)
+            for e in range(2):
+                first = ROW0 + QUAD * e
+                nc.scalar.dma_start(win[first : first + 16, :], rows[e])
+            scale_win.append(win)
+
 
         ident = sb.tile([P, P], F32, name="ident")
         make_identity(nc, ident[:])
 
-        nb_win = sb.tile([P, T], F32, name="nb_win", tag="nb_then_codes", align_bytes=64)
+        nb_win = sb.tile([P, T], F32, name="nb_win", tag="nb_slot", align_bytes=64)
         for b in range(banks):
             spread = ps.tile([P, per_bank, P], F32, name="spread%d" % b)
             for j in range(per_bank):
@@ -76,30 +77,30 @@ def tile_attend_neu_reglu_topk_kernel(tc, qT, k_words, k_scales, c_words, c_scal
         picked_scales = sb.tile([P, 2, N], U8, name="picked_scales", align_bytes=64)
         for i in range(2):
             nc.vector.tensor_copy(picked_scales[:, i, :], scale_win[i][:].bitcast(U8).indirect(offsets[:]))
-        planes = sb.tile([P, PASSES, 2, N], U8, name="planes", align_bytes=64)
+        c_win = sb.tile([P, T], I32, name="c_win", tag="k_scale_slot", align_bytes=64)
+        nc.sync.dma_start(c_win[:], c_words[0].rearrange("p t b -> p (t b)").bitcast(I32))
+
+        planes = shared.tile([P, PASSES, 2, N], U8, name="planes", align_bytes=64, offset=0)
         for o in range(PASSES):
             for h in range(2):
                 first = ROW0 + 4 * (2 * o + h)
-                nc.sync.dma_start(
+                nc.scalar.dma_start(
                     planes[HALF * h : HALF * (h + 1), o].rearrange("p i n -> p (i n)").bitcast(I32),
                     picked_scales[first : first + HALF].rearrange("p i n -> p (i n)").bitcast(I32),
                 )
 
-        c_win = sb.tile([P, T], I32, name="c_win", tag="c_first", align_bytes=64)
-        nc.sync.dma_start(c_win[:], c_words[0].rearrange("p t b -> p (t b)").bitcast(I32))
-
-        q_bf = sb.tile([P, PASSES, NQ, PACK], BF16, name="q_bf", tag="nb_then_q", align_bytes=64)
+        q_bf = shared.tile([P, PASSES, NQ, PACK], BF16, name="q_bf", align_bytes=64, offset=2 * PASSES * N)
         for o in range(PASSES):
             nc.scalar.activation(q_bf[:, o], q_raw[:, o].rearrange("p j w -> p w j"), ACT.Copy)
 
-        k_pairs = sb.tile([P, N], U32, name="k_pairs", align_bytes=64)
+        k_pairs = sb.tile([P, N], U32, name="k_pairs", tag="c_scale_slot", align_bytes=64)
         nc.vector.tensor_copy(k_pairs[:], k_win[:].bitcast(U32).indirect(offsets[:]))
         nb_picked = sb.tile([P, N], F32, name="nb_picked", align_bytes=64)
         nc.vector.tensor_copy(nb_picked[:], nb_win[:].indirect(offsets[:]))
-        k_split = sb.tile([P, PASSES, 2 * N], U8, name="k_split", align_bytes=64)
+        k_split = sb.tile([P, PASSES, 2 * N], U8, name="k_split", tag="nb_slot", align_bytes=64)
         nc.vector.tensor_copy(k_split[:].bitcast(U16), k_pairs[:].bitcast(U16).rearrange("p (n o) -> p o n", o=PASSES))
 
-        q_codes = sb.tile([P, PASSES * NQ], U32, name="q_codes", tag="nb_then_codes", align_bytes=64)
+        q_codes = sb.tile([P, PASSES * NQ], U32, name="q_codes", tag="c_scale_slot", align_bytes=64)
         q_scales = sb.tile([P, PASSES * NQ], U8, name="q_scales", align_bytes=64)
         nc.vector.quantize_mx(
             out=q_codes[:].bitcast(FP8X4), scales=q_scales[:], in_=q_bf[:].rearrange("p o w j -> p (o w j)")
@@ -120,17 +121,15 @@ def tile_attend_neu_reglu_topk_kernel(tc, qT, k_words, k_scales, c_words, c_scal
         a = ps.tile([P, N], F32, name="a")
         product(a[:], lambda o: k_split[:, o, :], lambda o: planes[:, o, 0, :])
 
-        c_pairs = []
+        c_pairs = shared.tile([P, PARTS, PART], U32, name="c_pairs", align_bytes=64, offset=2 * PASSES * N)
         for s in range(PARTS):
-            pairs = sb.tile([P, PART], U32, name="c_pairs%d" % s, tag=("nb_then_q", "c_pairs")[s], align_bytes=64)
             cols = slice(s * PART // 16, (s + 1) * PART // 16)
-            nc.vector.tensor_copy(pairs[:], c_win[:].bitcast(U32).indirect(offsets[:, cols]))
-            c_pairs.append(pairs)
+            nc.vector.tensor_copy(c_pairs[:, s, :], c_win[:].bitcast(U32).indirect(offsets[:, cols]))
         z = []
         for s in range(PARTS):
             split = sb.tile([P, PASSES, 2 * PART], U8, name="c_split%d" % s, align_bytes=64)
             nc.vector.tensor_copy(
-                split[:].bitcast(U16), c_pairs[s][:].bitcast(U16).rearrange("p (n o) -> p o n", o=PASSES)
+                split[:].bitcast(U16), c_pairs[:, s, :].bitcast(U16).rearrange("p (n o) -> p o n", o=PASSES)
             )
             acc = ps.tile([P, PART], F32, name="z%d" % s)
             for c in range(PART // P):

@@ -39,31 +39,36 @@ def tile_attend_neu_reglu_topk_kernel(tc, qT, k_words, k_scales, c_words, c_scal
         nc.sync.dma_start(offsets[:], offs)
 
         banks, per_bank = T // BANK, BANK // P
-        nb_cols = shared.tile([P, banks, per_bank], F32, name="nb_cols", offset=2 * PASSES * N - 32)
+        nb_cols = sb.tile([P, banks, per_bank], F32, name="nb_cols", tag="q_slot", align_bytes=64)
         nc.sync.dma_start(nb_cols[:], nb[0].rearrange("(b n j) -> n b j", b=banks, j=per_bank))
 
-        k_win = sb.tile([P, T], I32, name="k_win", align_bytes=64)
-        nc.sync.dma_start(k_win[:], k_words[0].rearrange("p t b -> p (t b)").bitcast(I32))
-        q_raw = sb.tile([P, PASSES, PACK, NQ], F32, name="q_raw")
-        nc.sync.dma_start(
-            q_raw[:].rearrange("p o j w -> p o (j w)"),
-            qT[0].rearrange("(o p j) w -> p o (j w)", o=PASSES, j=PACK),
-        )
         scale_win = []
         for name, src in (("k", k_scales), ("c", c_scales)):
-            win = sb.tile([P, T // 4], I32, name=name + "_scale_win", tag=name + "_scale_slot", align_bytes=64)
+            win = sb.tile([P, T // 4], I32, name=name + "_scale_win", align_bytes=64)
             nc.vector.memset(win[:], 0)
             rows = src.bitcast(I32).rearrange("o (h e r) t -> e (o h) r t", h=2, e=2)
             for e in range(2):
                 first = ROW0 + QUAD * e
-                nc.scalar.dma_start(win[first : first + 16, :], rows[e])
+                nc.sync.dma_start(win[first : first + 16, :], rows[e])
             scale_win.append(win)
 
+        planes = sb.tile([P, PASSES, 2 * N // 4], I32, name="planes", align_bytes=64)
+        nc.vector.memset(planes[:], 0)
+
+        k_win = sb.tile([P, T], I32, name="k_win", align_bytes=64)
+        nc.sync.dma_start(k_win[:], k_words[0].rearrange("p t b -> p (t b)").bitcast(I32))
+        q_raw = shared.tile([P, PASSES, PACK, NQ], F32, name="q_raw", align_bytes=64, offset=0)
+        nc.sync.dma_start(
+            q_raw[:].rearrange("p o j w -> p o (j w)"),
+            qT[0].rearrange("(o p j) w -> p o (j w)", o=PASSES, j=PACK),
+        )
+        c_win = sb.tile([P, T], I32, name="c_win", tag="c_slot", align_bytes=64)
+        nc.sync.dma_start(c_win[:], c_words[0].rearrange("p t b -> p (t b)").bitcast(I32))
 
         ident = sb.tile([P, P], F32, name="ident")
         make_identity(nc, ident[:])
 
-        nb_win = sb.tile([P, T], F32, name="nb_win", tag="nb_slot", align_bytes=64)
+        nb_win = sb.tile([P, T], F32, name="nb_win", align_bytes=64)
         for b in range(banks):
             spread = ps.tile([P, per_bank, P], F32, name="spread%d" % b)
             for j in range(per_bank):
@@ -77,30 +82,28 @@ def tile_attend_neu_reglu_topk_kernel(tc, qT, k_words, k_scales, c_words, c_scal
         picked_scales = sb.tile([P, 2, N], U8, name="picked_scales", align_bytes=64)
         for i in range(2):
             nc.vector.tensor_copy(picked_scales[:, i, :], scale_win[i][:].bitcast(U8).indirect(offsets[:]))
-        c_win = sb.tile([P, T], I32, name="c_win", tag="k_scale_slot", align_bytes=64)
-        nc.sync.dma_start(c_win[:], c_words[0].rearrange("p t b -> p (t b)").bitcast(I32))
-
-        planes = shared.tile([P, PASSES, 2, N], U8, name="planes", align_bytes=64, offset=0)
         for o in range(PASSES):
             for h in range(2):
                 first = ROW0 + 4 * (2 * o + h)
-                nc.scalar.dma_start(
-                    planes[HALF * h : HALF * (h + 1), o].rearrange("p i n -> p (i n)").bitcast(I32),
-                    picked_scales[first : first + HALF].rearrange("p i n -> p (i n)").bitcast(I32),
-                )
+                spans = [(0, HALF)] if (o, h) == (PASSES - 1, 1) else [(0, 4), (QUAD, 4)]
+                for skip, count in spans:
+                    nc.sync.dma_start(
+                        planes[HALF * h + skip : HALF * h + skip + count, o, :],
+                        picked_scales[first + skip : first + skip + count].rearrange("p i n -> p (i n)").bitcast(I32),
+                    )
 
-        q_bf = shared.tile([P, PASSES, NQ, PACK], BF16, name="q_bf", align_bytes=64, offset=2 * PASSES * N)
+        q_bf = sb.tile([P, PASSES, NQ, PACK], BF16, name="q_bf", tag="q_slot", align_bytes=64)
         for o in range(PASSES):
             nc.scalar.activation(q_bf[:, o], q_raw[:, o].rearrange("p j w -> p w j"), ACT.Copy)
 
-        k_pairs = sb.tile([P, N], U32, name="k_pairs", tag="c_scale_slot", align_bytes=64)
+        k_pairs = sb.tile([P, N], U32, name="k_pairs", align_bytes=64)
         nc.vector.tensor_copy(k_pairs[:], k_win[:].bitcast(U32).indirect(offsets[:]))
         nb_picked = sb.tile([P, N], F32, name="nb_picked", align_bytes=64)
         nc.vector.tensor_copy(nb_picked[:], nb_win[:].indirect(offsets[:]))
-        k_split = sb.tile([P, PASSES, 2 * N], U8, name="k_split", tag="nb_slot", align_bytes=64)
+        k_split = shared.tile([P, PASSES, 2 * N], U8, name="k_split", align_bytes=64, offset=0)
         nc.vector.tensor_copy(k_split[:].bitcast(U16), k_pairs[:].bitcast(U16).rearrange("p (n o) -> p o n", o=PASSES))
 
-        q_codes = sb.tile([P, PASSES * NQ], U32, name="q_codes", tag="c_scale_slot", align_bytes=64)
+        q_codes = sb.tile([P, PASSES * NQ], U32, name="q_codes", align_bytes=64)
         q_scales = sb.tile([P, PASSES * NQ], U8, name="q_scales", align_bytes=64)
         nc.vector.quantize_mx(
             out=q_codes[:].bitcast(FP8X4), scales=q_scales[:], in_=q_bf[:].rearrange("p o w j -> p (o w j)")
@@ -119,9 +122,9 @@ def tile_attend_neu_reglu_topk_kernel(tc, qT, k_words, k_scales, c_words, c_scal
                 )
 
         a = ps.tile([P, N], F32, name="a")
-        product(a[:], lambda o: k_split[:, o, :], lambda o: planes[:, o, 0, :])
+        product(a[:], lambda o: k_split[:, o, :], lambda o: planes[:, o, :].bitcast(U8)[:, :N])
 
-        c_pairs = shared.tile([P, PARTS, PART], U32, name="c_pairs", align_bytes=64, offset=2 * PASSES * N)
+        c_pairs = shared.tile([P, PARTS, PART], U32, name="c_pairs", align_bytes=64, offset=PASSES * 2 * N)
         for s in range(PARTS):
             cols = slice(s * PART // 16, (s + 1) * PART // 16)
             nc.vector.tensor_copy(c_pairs[:, s, :], c_win[:].bitcast(U32).indirect(offsets[:, cols]))
@@ -137,11 +140,11 @@ def tile_attend_neu_reglu_topk_kernel(tc, qT, k_words, k_scales, c_words, c_scal
                 product(
                     acc[:, c * P : (c + 1) * P],
                     lambda o: split[:, o, 2 * c * P : 2 * (c + 1) * P],
-                    lambda o: planes[:, o, 1, first : first + P],
+                    lambda o: planes[:, o, :].bitcast(U8)[:, N + first : N + first + P],
                 )
             z.append(acc)
 
-        gate = sb.tile([P, N], F32, name="gate")
+        gate = sb.tile([P, N], F32, name="gate", tag="c_slot", align_bytes=64)
         nc.vector.tensor_tensor(gate[:], a[:], nb_picked[:], ALU.add)
         for s in range(PARTS):
             cols = slice(s * PART, (s + 1) * PART)

@@ -20,12 +20,13 @@ ALU = mybir.AluOpType
 P = 128
 PACK = 4
 PASSES = D // (P * PACK)
-HALF = P // 2
 QUAD = 32
-ROW0 = 32
-BANK = 512
+QUADS = P // QUAD
+ROW0 = P - QUAD
+LAST = P - 1
 PARTS = 2
 PART = N // PARTS
+BLOCKS = N // P
 
 
 def tile_attend_neu_reglu_topk_kernel(tc, qT, k_words, k_scales, c_words, c_scales, nb, offs, out):
@@ -38,93 +39,93 @@ def tile_attend_neu_reglu_topk_kernel(tc, qT, k_words, k_scales, c_words, c_scal
         offsets = sb.tile([P, N // 16], U16, name="offsets")
         nc.sync.dma_start(offsets[:], offs)
 
-        banks, per_bank = T // BANK, BANK // P
-        nb_cols = sb.tile([P, banks, per_bank], F32, name="nb_cols", tag="q_slot", align_bytes=64)
-        nc.sync.dma_start(nb_cols[:], nb[0].rearrange("(b n j) -> n b j", b=banks, j=per_bank))
-
         scale_win = []
-        for name, src in (("k", k_scales), ("c", c_scales)):
-            win = sb.tile([P, T // 4], I32, name=name + "_scale_win", align_bytes=64)
-            nc.vector.memset(win[:], 0)
-            rows = src.bitcast(I32).rearrange("o (h e r) t -> e (o h) r t", h=2, e=2)
-            for e in range(2):
-                first = ROW0 + QUAD * e
-                nc.sync.dma_start(win[first : first + 16, :], rows[e])
+        for name, src, tag in (("k", k_scales, "c_slot"), ("c", c_scales, "c_scale_slot")):
+            win = sb.tile([P, T // 4], I32, name=name + "_scale_win", tag=tag, align_bytes=64)
+            nc.gpsimd.memset(win[:ROW0, :], 0)
+            nc.sync.dma_start(win[ROW0:, :], src.bitcast(I32).rearrange("o f t -> (o f) t"))
             scale_win.append(win)
 
-        planes = sb.tile([P, PASSES, 2 * N // 4], I32, name="planes", align_bytes=64)
-        nc.vector.memset(planes[:], 0)
+        nb_win = sb.tile([P, T], F32, name="nb_win", align_bytes=64)
+        nc.vector.memset(nb_win[:LAST, :], 0.0)
+        nc.sync.dma_start(nb_win[LAST:, :], nb[0:1, :])
+
+        planes = sb.tile([P, PASSES, 2, N // 4], I32, name="planes", align_bytes=64)
+        nc.gpsimd.memset(planes[:], 0)
 
         k_win = sb.tile([P, T], I32, name="k_win", align_bytes=64)
-        nc.sync.dma_start(k_win[:], k_words[0].rearrange("p t b -> p (t b)").bitcast(I32))
         q_raw = shared.tile([P, PASSES, PACK, NQ], F32, name="q_raw", align_bytes=64, offset=0)
-        nc.sync.dma_start(
-            q_raw[:].rearrange("p o j w -> p o (j w)"),
-            qT[0].rearrange("(o p j) w -> p o (j w)", o=PASSES, j=PACK),
-        )
-        c_win = sb.tile([P, T], I32, name="c_win", tag="c_slot", align_bytes=64)
-        nc.sync.dma_start(c_win[:], c_words[0].rearrange("p t b -> p (t b)").bitcast(I32))
+        q_rows = qT[0].rearrange("(o p j) w -> o p j w", o=PASSES, j=PACK)
+        nc.sync.dma_start(q_raw[:, 0], q_rows[0])
+        nc.sync.dma_start(k_win[:], k_words[0].rearrange("p t b -> p (t b)").bitcast(I32))
+        nc.sync.dma_start(q_raw[:, 1], q_rows[1])
 
         ident = sb.tile([P, P], F32, name="ident")
         make_identity(nc, ident[:])
 
-        nb_win = sb.tile([P, T], F32, name="nb_win", align_bytes=64)
-        for b in range(banks):
-            spread = ps.tile([P, per_bank, P], F32, name="spread%d" % b)
-            for j in range(per_bank):
-                nc.tensor.transpose(spread[:, j, :], nb_cols[:, b, j : j + 1].to_broadcast([P, P]), ident[:])
-            nc.scalar.activation(
-                nb_win[:, b * BANK : (b + 1) * BANK].rearrange("p (n j) -> p n j", j=per_bank),
-                spread[:].rearrange("p j n -> p n j"),
-                ACT.Copy,
+        picked_scales = sb.tile([P, 2, N], U8, name="picked_scales", align_bytes=64)
+
+        def move_scales(o, quad, tables):
+            first = ROW0 + 16 * o + 4 * quad
+            nc.sync.dma_start(
+                planes[QUAD * quad : QUAD * quad + 4, o, tables].rearrange("p i n -> p (i n)"),
+                picked_scales[first : first + 4, tables].rearrange("p i n -> p (i n)").bitcast(I32),
             )
 
-        picked_scales = sb.tile([P, 2, N], U8, name="picked_scales", align_bytes=64)
-        for i in range(2):
-            nc.vector.tensor_copy(picked_scales[:, i, :], scale_win[i][:].bitcast(U8).indirect(offsets[:]))
+        nc.vector.tensor_copy(picked_scales[:, 0, :], scale_win[0][:].bitcast(U8).indirect(offsets[:]))
+        move_scales(PASSES - 1, QUADS - 1, slice(0, 1))
+        c_win = sb.tile([P, T], I32, name="c_win", tag="c_slot", align_bytes=64)
+        nc.sync.dma_start(c_win[:], c_words[0].rearrange("p t b -> p (t b)").bitcast(I32))
+        nc.vector.tensor_copy(picked_scales[:, 1, :], scale_win[1][:].bitcast(U8).indirect(offsets[:]))
         for o in range(PASSES):
-            for h in range(2):
-                first = ROW0 + 4 * (2 * o + h)
-                spans = [(0, HALF)] if (o, h) == (PASSES - 1, 1) else [(0, 4), (QUAD, 4)]
-                for skip, count in spans:
-                    nc.sync.dma_start(
-                        planes[HALF * h + skip : HALF * h + skip + count, o, :],
-                        picked_scales[first + skip : first + skip + count].rearrange("p i n -> p (i n)").bitcast(I32),
-                    )
+            for quad in range(QUADS):
+                last = (o, quad) == (PASSES - 1, QUADS - 1)
+                move_scales(o, quad, slice(1, 2) if last else slice(0, 2))
 
-        q_bf = sb.tile([P, PASSES, NQ, PACK], BF16, name="q_bf", tag="q_slot", align_bytes=64)
+        nb_picked = sb.tile([P, N], F32, name="nb_picked", align_bytes=64)
+        nc.vector.tensor_copy(nb_picked[:], nb_win[:].indirect(offsets[:]))
+        k_pairs = sb.tile([P, N], U32, name="k_pairs", align_bytes=64)
+        nc.vector.tensor_copy(k_pairs[:], k_win[:].bitcast(U32).indirect(offsets[:]))
+
+        q_bf = sb.tile([P, PASSES, NQ, PACK], BF16, name="q_bf", align_bytes=64)
         for o in range(PASSES):
             nc.scalar.activation(q_bf[:, o], q_raw[:, o].rearrange("p j w -> p w j"), ACT.Copy)
 
-        k_pairs = sb.tile([P, N], U32, name="k_pairs", align_bytes=64)
-        nc.vector.tensor_copy(k_pairs[:], k_win[:].bitcast(U32).indirect(offsets[:]))
-        nb_picked = sb.tile([P, N], F32, name="nb_picked", align_bytes=64)
-        nc.vector.tensor_copy(nb_picked[:], nb_win[:].indirect(offsets[:]))
-        k_split = shared.tile([P, PASSES, 2 * N], U8, name="k_split", align_bytes=64, offset=0)
-        nc.vector.tensor_copy(k_split[:].bitcast(U16), k_pairs[:].bitcast(U16).rearrange("p (n o) -> p o n", o=PASSES))
+        turned = ps.tile([P, BLOCKS, P], F32, name="turned")
+        for j in range(BLOCKS):
+            nc.tensor.transpose(turned[:, j, :], nb_picked[:, j * P : (j + 1) * P], ident[:])
+        nb_cols = shared.tile([P, BLOCKS], F32, name="nb_cols", align_bytes=64, offset=PASSES * 2 * N)
+        nc.scalar.activation(nb_cols[:], turned[:, :, LAST], ACT.Copy)
+        spread = ps.tile([P, BLOCKS, P], F32, name="spread")
+        for j in range(BLOCKS):
+            nc.tensor.transpose(spread[:, j, :], nb_cols[:, j : j + 1].to_broadcast([P, P]), ident[:])
+        bias = sb.tile([P, N], F32, name="bias")
+        nc.scalar.activation(bias[:], spread[:].rearrange("p j n -> p (j n)"), ACT.Copy)
 
         q_codes = sb.tile([P, PASSES * NQ], U32, name="q_codes", align_bytes=64)
         q_scales = sb.tile([P, PASSES * NQ], U8, name="q_scales", align_bytes=64)
         nc.vector.quantize_mx(
             out=q_codes[:].bitcast(FP8X4), scales=q_scales[:], in_=q_bf[:].rearrange("p o w j -> p (o w j)")
         )
+        k_split = shared.tile([P, PASSES, 2 * N], U8, name="k_split", align_bytes=64, offset=0)
+        nc.vector.tensor_copy(k_split[:].bitcast(U16), k_pairs[:].bitcast(U16).rearrange("p (n o) -> p o n", o=PASSES))
 
         def product(acc, words, scales):
-            for o in range(PASSES):
+            for o in reversed(range(PASSES)):
                 nc.tensor.matmul_mx(
                     out=acc,
                     lhsT=q_codes[:, o * NQ : (o + 1) * NQ].bitcast(FP8X4),
                     lhsT_scale=q_scales[:, o * NQ : (o + 1) * NQ],
                     rhs=words(o).bitcast(FP4X4),
                     rhs_scale=scales(o),
-                    start=(o == 0),
-                    stop=(o == PASSES - 1),
+                    start=(o == PASSES - 1),
+                    stop=(o == 0),
                 )
 
         a = ps.tile([P, N], F32, name="a")
-        product(a[:], lambda o: k_split[:, o, :], lambda o: planes[:, o, :].bitcast(U8)[:, :N])
+        product(a[:], lambda o: k_split[:, o, :], lambda o: planes[:, o, 0, :].bitcast(U8))
 
-        c_pairs = shared.tile([P, PARTS, PART], U32, name="c_pairs", align_bytes=64, offset=PASSES * 2 * N)
+        c_pairs = shared.tile([P, PARTS, PART], U32, name="c_pairs", align_bytes=64, offset=PASSES * 2 * N + 64)
         for s in range(PARTS):
             cols = slice(s * PART // 16, (s + 1) * PART // 16)
             nc.vector.tensor_copy(c_pairs[:, s, :], c_win[:].bitcast(U32).indirect(offsets[:, cols]))
@@ -140,12 +141,12 @@ def tile_attend_neu_reglu_topk_kernel(tc, qT, k_words, k_scales, c_words, c_scal
                 product(
                     acc[:, c * P : (c + 1) * P],
                     lambda o: split[:, o, 2 * c * P : 2 * (c + 1) * P],
-                    lambda o: planes[:, o, :].bitcast(U8)[:, N + first : N + first + P],
+                    lambda o: planes[:, o, 1, :].bitcast(U8)[:, first : first + P],
                 )
             z.append(acc)
 
         gate = sb.tile([P, N], F32, name="gate", tag="c_slot", align_bytes=64)
-        nc.vector.tensor_tensor(gate[:], a[:], nb_picked[:], ALU.add)
+        nc.vector.tensor_tensor(gate[:], a[:], bias[:], ALU.add)
         for s in range(PARTS):
             cols = slice(s * PART, (s + 1) * PART)
             result = sb.tile([P, PART], F32, name="result%d" % s)

@@ -23,10 +23,11 @@ PASSES = D // (P * PACK)
 QUAD = 32
 QUADS = P // QUAD
 ROW0 = P - QUAD
-LAST = P - 1
 PARTS = 2
 PART = N // PARTS
-BLOCKS = N // P
+BANK = 512
+BANKS = T // BANK
+BLOCKS = BANK // P
 
 
 def tile_attend_neu_reglu_topk_kernel(tc, qT, k_words, k_scales, c_words, c_scales, nb, offs, out):
@@ -42,26 +43,37 @@ def tile_attend_neu_reglu_topk_kernel(tc, qT, k_words, k_scales, c_words, c_scal
         scale_win = []
         for name, src, tag in (("k", k_scales, "c_slot"), ("c", c_scales, "c_scale_slot")):
             win = sb.tile([P, T // 4], I32, name=name + "_scale_win", tag=tag, align_bytes=64)
-            nc.gpsimd.memset(win[:ROW0, :], 0)
+            nc.vector.memset(win[:ROW0, :], 0)
             nc.sync.dma_start(win[ROW0:, :], src.bitcast(I32).rearrange("o f t -> (o f) t"))
             scale_win.append(win)
 
-        nb_win = sb.tile([P, T], F32, name="nb_win", align_bytes=64)
-        nc.vector.memset(nb_win[:LAST, :], 0.0)
-        nc.sync.dma_start(nb_win[LAST:, :], nb[0:1, :])
+        nb_cols = sb.tile([P, BANKS, BLOCKS], F32, name="nb_cols", tag="q_slot", align_bytes=64)
+        nc.sync.dma_start(nb_cols[:], nb[0].rearrange("(b n j) -> n b j", b=BANKS, j=BLOCKS))
 
         planes = sb.tile([P, PASSES, 2, N // 4], I32, name="planes", align_bytes=64)
-        nc.gpsimd.memset(planes[:], 0)
+        nc.vector.memset(planes[:], 0)
 
         k_win = sb.tile([P, T], I32, name="k_win", align_bytes=64)
         q_raw = shared.tile([P, PASSES, PACK, NQ], F32, name="q_raw", align_bytes=64, offset=0)
-        q_rows = qT[0].rearrange("(o p j) w -> o p j w", o=PASSES, j=PACK)
-        nc.sync.dma_start(q_raw[:, 0], q_rows[0])
         nc.sync.dma_start(k_win[:], k_words[0].rearrange("p t b -> p (t b)").bitcast(I32))
-        nc.sync.dma_start(q_raw[:, 1], q_rows[1])
+        nc.sync.dma_start(
+            q_raw[:].rearrange("p o j w -> p o (j w)"),
+            qT[0].rearrange("(o p j) w -> p o (j w)", o=PASSES, j=PACK),
+        )
 
         ident = sb.tile([P, P], F32, name="ident")
         make_identity(nc, ident[:])
+
+        nb_win = sb.tile([P, T], F32, name="nb_win", align_bytes=64)
+        for b in range(BANKS):
+            spread = ps.tile([P, BLOCKS, P], F32, name="spread%d" % b)
+            for j in range(BLOCKS):
+                nc.tensor.transpose(spread[:, j, :], nb_cols[:, b, j : j + 1].to_broadcast([P, P]), ident[:])
+            nc.scalar.activation(
+                nb_win[:, b * BANK : (b + 1) * BANK].rearrange("p (n j) -> p n j", j=BLOCKS),
+                spread[:].rearrange("p j n -> p n j"),
+                ACT.Copy,
+            )
 
         picked_scales = sb.tile([P, 2, N], U8, name="picked_scales", align_bytes=64)
 
@@ -82,33 +94,28 @@ def tile_attend_neu_reglu_topk_kernel(tc, qT, k_words, k_scales, c_words, c_scal
                 last = (o, quad) == (PASSES - 1, QUADS - 1)
                 move_scales(o, quad, slice(1, 2) if last else slice(0, 2))
 
+        k_pairs = sb.tile([P, PARTS, PART], U32, name="k_pairs", align_bytes=64)
+        for s in range(PARTS):
+            cols = slice(s * PART // 16, (s + 1) * PART // 16)
+            nc.vector.tensor_copy(k_pairs[:, s, :], k_win[:].bitcast(U32).indirect(offsets[:, cols]))
+        k_split = sb.tile([P, PASSES, 2 * N], U8, name="k_split", align_bytes=64)
+        for s in range(PARTS):
+            nc.vector.tensor_copy(
+                k_split[:, :, 2 * s * PART : 2 * (s + 1) * PART].bitcast(U16),
+                k_pairs[:, s, :].bitcast(U16).rearrange("p (n o) -> p o n", o=PASSES),
+            )
         nb_picked = sb.tile([P, N], F32, name="nb_picked", align_bytes=64)
         nc.vector.tensor_copy(nb_picked[:], nb_win[:].indirect(offsets[:]))
-        k_pairs = sb.tile([P, N], U32, name="k_pairs", align_bytes=64)
-        nc.vector.tensor_copy(k_pairs[:], k_win[:].bitcast(U32).indirect(offsets[:]))
 
-        q_bf = sb.tile([P, PASSES, NQ, PACK], BF16, name="q_bf", align_bytes=64)
+        q_bf = sb.tile([P, PASSES, NQ, PACK], BF16, name="q_bf", tag="q_slot", align_bytes=64)
         for o in range(PASSES):
             nc.scalar.activation(q_bf[:, o], q_raw[:, o].rearrange("p j w -> p w j"), ACT.Copy)
-
-        turned = ps.tile([P, BLOCKS, P], F32, name="turned")
-        for j in range(BLOCKS):
-            nc.tensor.transpose(turned[:, j, :], nb_picked[:, j * P : (j + 1) * P], ident[:])
-        nb_cols = shared.tile([P, BLOCKS], F32, name="nb_cols", align_bytes=64, offset=PASSES * 2 * N)
-        nc.scalar.activation(nb_cols[:], turned[:, :, LAST], ACT.Copy)
-        spread = ps.tile([P, BLOCKS, P], F32, name="spread")
-        for j in range(BLOCKS):
-            nc.tensor.transpose(spread[:, j, :], nb_cols[:, j : j + 1].to_broadcast([P, P]), ident[:])
-        bias = sb.tile([P, N], F32, name="bias")
-        nc.scalar.activation(bias[:], spread[:].rearrange("p j n -> p (j n)"), ACT.Copy)
 
         q_codes = sb.tile([P, PASSES * NQ], U32, name="q_codes", align_bytes=64)
         q_scales = sb.tile([P, PASSES * NQ], U8, name="q_scales", align_bytes=64)
         nc.vector.quantize_mx(
             out=q_codes[:].bitcast(FP8X4), scales=q_scales[:], in_=q_bf[:].rearrange("p o w j -> p (o w j)")
         )
-        k_split = shared.tile([P, PASSES, 2 * N], U8, name="k_split", align_bytes=64, offset=0)
-        nc.vector.tensor_copy(k_split[:].bitcast(U16), k_pairs[:].bitcast(U16).rearrange("p (n o) -> p o n", o=PASSES))
 
         def product(acc, words, scales):
             for o in reversed(range(PASSES)):
@@ -125,7 +132,7 @@ def tile_attend_neu_reglu_topk_kernel(tc, qT, k_words, k_scales, c_words, c_scal
         a = ps.tile([P, N], F32, name="a")
         product(a[:], lambda o: k_split[:, o, :], lambda o: planes[:, o, 0, :].bitcast(U8))
 
-        c_pairs = shared.tile([P, PARTS, PART], U32, name="c_pairs", align_bytes=64, offset=PASSES * 2 * N + 64)
+        c_pairs = shared.tile([P, PARTS, PART], U32, name="c_pairs", align_bytes=64, offset=0)
         for s in range(PARTS):
             cols = slice(s * PART // 16, (s + 1) * PART // 16)
             nc.vector.tensor_copy(c_pairs[:, s, :], c_win[:].bitcast(U32).indirect(offsets[:, cols]))
@@ -146,7 +153,9 @@ def tile_attend_neu_reglu_topk_kernel(tc, qT, k_words, k_scales, c_words, c_scal
             z.append(acc)
 
         gate = sb.tile([P, N], F32, name="gate", tag="c_slot", align_bytes=64)
-        nc.vector.tensor_tensor(gate[:], a[:], bias[:], ALU.add)
+        for s in range(PARTS):
+            cols = slice(s * PART, (s + 1) * PART)
+            nc.vector.tensor_tensor(gate[:, cols], a[:, cols], nb_picked[:, cols], ALU.add)
         for s in range(PARTS):
             cols = slice(s * PART, (s + 1) * PART)
             result = sb.tile([P, PART], F32, name="result%d" % s)

@@ -41,8 +41,8 @@ def tile_attend_neu_reglu_topk_kernel(tc, qT, k_words, k_scales, c_words, c_scal
         nc.sync.dma_start(offsets[:], offs)
 
         scale_win = []
-        for name, src, tag in (("k", k_scales, "c_slot"), ("c", c_scales, "c_scale_slot")):
-            win = sb.tile([P, T // 4], I32, name=name + "_scale_win", tag=tag, align_bytes=64)
+        for name, src in (("k", k_scales), ("c", c_scales)):
+            win = sb.tile([P, T // 4], I32, name=name + "_scale_win", align_bytes=64)
             nc.vector.memset(win[:ROW0, :], 0)
             nc.sync.dma_start(win[ROW0:, :], src.bitcast(I32).rearrange("o f t -> (o f) t"))
             scale_win.append(win)
@@ -60,6 +60,8 @@ def tile_attend_neu_reglu_topk_kernel(tc, qT, k_words, k_scales, c_words, c_scal
             q_raw[:].rearrange("p o j w -> p o (j w)"),
             qT[0].rearrange("(o p j) w -> p o (j w)", o=PASSES, j=PACK),
         )
+        c_win = sb.tile([P, T], I32, name="c_win", tag="c_slot", align_bytes=64)
+        nc.sync.dma_start(c_win[:], c_words[0].rearrange("p t b -> p (t b)").bitcast(I32))
 
         ident = sb.tile([P, P], F32, name="ident")
         make_identity(nc, ident[:])
@@ -76,23 +78,16 @@ def tile_attend_neu_reglu_topk_kernel(tc, qT, k_words, k_scales, c_words, c_scal
             )
 
         picked_scales = sb.tile([P, 2, N], U8, name="picked_scales", align_bytes=64)
-
-        def move_scales(o, quad, tables):
-            first = ROW0 + 16 * o + 4 * quad
-            nc.sync.dma_start(
-                planes[QUAD * quad : QUAD * quad + 4, o, tables].rearrange("p i n -> p (i n)"),
-                picked_scales[first : first + 4, tables].rearrange("p i n -> p (i n)").bitcast(I32),
-            )
-
-        nc.vector.tensor_copy(picked_scales[:, 0, :], scale_win[0][:].bitcast(U8).indirect(offsets[:]))
-        move_scales(PASSES - 1, QUADS - 1, slice(0, 1))
-        c_win = sb.tile([P, T], I32, name="c_win", tag="c_slot", align_bytes=64)
-        nc.sync.dma_start(c_win[:], c_words[0].rearrange("p t b -> p (t b)").bitcast(I32))
-        nc.vector.tensor_copy(picked_scales[:, 1, :], scale_win[1][:].bitcast(U8).indirect(offsets[:]))
+        for i in range(2):
+            nc.vector.tensor_copy(picked_scales[:, i, :], scale_win[i][:].bitcast(U8).indirect(offsets[:]))
         for o in range(PASSES):
             for quad in range(QUADS):
-                last = (o, quad) == (PASSES - 1, QUADS - 1)
-                move_scales(o, quad, slice(1, 2) if last else slice(0, 2))
+                first = ROW0 + 16 * o + 4 * quad
+                queue = nc.gpsimd if (o, quad) == (PASSES - 1, QUADS - 1) else nc.sync
+                queue.dma_start(
+                    planes[QUAD * quad : QUAD * quad + 4, o].rearrange("p i n -> p (i n)"),
+                    picked_scales[first : first + 4].rearrange("p i n -> p (i n)").bitcast(I32),
+                )
 
         k_pairs = sb.tile([P, PARTS, PART], U32, name="k_pairs", align_bytes=64)
         for s in range(PARTS):

@@ -38,17 +38,17 @@ def tile_attend_neu_reglu_topk_kernel(tc, qT, k_words, k_scales, c_words, c_scal
         ps = ctx.enter_context(tc.psum_pool(name="ps", bufs=1))
 
         offsets = sb.tile([P, N // 16], U16, name="offsets")
-        nc.sync.dma_start(offsets[:], offs)
-
         scale_win = []
         for name, src in (("k", k_scales), ("c", c_scales)):
             win = sb.tile([P, T // 4], I32, name=name + "_scale_win", align_bytes=64)
             nc.vector.memset(win[:ROW0, :], 0)
             nc.sync.dma_start(win[ROW0:, :], src.bitcast(I32).rearrange("o f t -> (o f) t"))
             scale_win.append(win)
+            if name == "k":
+                nc.sync.dma_start(offsets[:], offs)
 
         nb_cols = sb.tile([P, BANKS, BLOCKS], F32, name="nb_cols", tag="q_slot", align_bytes=64)
-        nc.sync.dma_start(nb_cols[:], nb[0].rearrange("(b n j) -> n b j", b=BANKS, j=BLOCKS))
+        nc.sync.dma_start(nb_cols[:], nb[0].rearrange("(n b j) -> n b j", b=BANKS, j=BLOCKS))
 
         planes = sb.tile([P, PASSES, 2, N // 4], I32, name="planes", align_bytes=64)
         nc.vector.memset(planes[:], 0)
@@ -72,7 +72,7 @@ def tile_attend_neu_reglu_topk_kernel(tc, qT, k_words, k_scales, c_words, c_scal
             for j in range(BLOCKS):
                 nc.tensor.transpose(spread[:, j, :], nb_cols[:, b, j : j + 1].to_broadcast([P, P]), ident[:])
             nc.scalar.activation(
-                nb_win[:, b * BANK : (b + 1) * BANK].rearrange("p (n j) -> p n j", j=BLOCKS),
+                nb_win[:].rearrange("p (n b j) -> p b n j", b=BANKS, j=BLOCKS)[:, b],
                 spread[:].rearrange("p j n -> p n j"),
                 ACT.Copy,
             )
@@ -104,7 +104,10 @@ def tile_attend_neu_reglu_topk_kernel(tc, qT, k_words, k_scales, c_words, c_scal
 
         q_bf = sb.tile([P, PASSES, NQ, PACK], BF16, name="q_bf", tag="q_slot", align_bytes=64)
         for o in range(PASSES):
-            nc.scalar.activation(q_bf[:, o], q_raw[:, o].rearrange("p j w -> p w j"), ACT.Copy)
+            nc.scalar.copy(
+                q_bf[:, o].rearrange("p (c i) j -> p c j i", i=PACK),
+                q_raw[:, o].rearrange("p j (c i) -> p c j i", i=PACK),
+            )
 
         q_codes = sb.tile([P, PASSES * NQ], U32, name="q_codes", align_bytes=64)
         q_scales = sb.tile([P, PASSES * NQ], U8, name="q_scales", align_bytes=64)
@@ -112,20 +115,20 @@ def tile_attend_neu_reglu_topk_kernel(tc, qT, k_words, k_scales, c_words, c_scal
             out=q_codes[:].bitcast(FP8X4), scales=q_scales[:], in_=q_bf[:].rearrange("p o w j -> p (o w j)")
         )
 
-        def product(acc, words, scales):
-            for o in reversed(range(PASSES)):
+        def product(acc, words, scales, order):
+            for o in order:
                 nc.tensor.matmul_mx(
                     out=acc,
                     lhsT=q_codes[:, o * NQ : (o + 1) * NQ].bitcast(FP8X4),
                     lhsT_scale=q_scales[:, o * NQ : (o + 1) * NQ],
                     rhs=words(o).bitcast(FP4X4),
                     rhs_scale=scales(o),
-                    start=(o == PASSES - 1),
-                    stop=(o == 0),
+                    start=(o == order[0]),
+                    stop=(o == order[-1]),
                 )
 
         a = ps.tile([P, N], F32, name="a")
-        product(a[:], lambda o: k_split[:, o, :], lambda o: planes[:, o, 0, :].bitcast(U8))
+        product(a[:], lambda o: k_split[:, o, :], lambda o: planes[:, o, 0, :].bitcast(U8), (0, 1))
 
         c_pairs = shared.tile([P, PARTS, PART], U32, name="c_pairs", align_bytes=64, offset=0)
         for s in range(PARTS):
@@ -134,9 +137,12 @@ def tile_attend_neu_reglu_topk_kernel(tc, qT, k_words, k_scales, c_words, c_scal
         z = []
         for s in range(PARTS):
             split = sb.tile([P, PASSES, 2 * PART], U8, name="c_split%d" % s, align_bytes=64)
-            nc.vector.tensor_copy(
-                split[:].bitcast(U16), c_pairs[:, s, :].bitcast(U16).rearrange("p (n o) -> p o n", o=PASSES)
-            )
+            step = P if s == 0 else PART
+            for n0 in range(0, PART, step):
+                nc.vector.tensor_copy(
+                    split[:, :, 2 * n0 : 2 * (n0 + step)].bitcast(U16),
+                    c_pairs[:, s, n0 : n0 + step].bitcast(U16).rearrange("p (n o) -> p o n", o=PASSES),
+                )
             acc = ps.tile([P, PART], F32, name="z%d" % s)
             for c in range(PART // P):
                 first = s * PART + c * P
@@ -144,6 +150,7 @@ def tile_attend_neu_reglu_topk_kernel(tc, qT, k_words, k_scales, c_words, c_scal
                     acc[:, c * P : (c + 1) * P],
                     lambda o: split[:, o, 2 * c * P : 2 * (c + 1) * P],
                     lambda o: planes[:, o, 1, :].bitcast(U8)[:, first : first + P],
+                    (1, 0),
                 )
             z.append(acc)
 

@@ -28,6 +28,10 @@ PART = N // PARTS
 BANK = 512
 BANKS = T // BANK
 BLOCKS = BANK // P
+Q_RAW_BYTES = PASSES * PACK * NQ * 4
+WIN_AT = {"c": Q_RAW_BYTES, "k": Q_RAW_BYTES + T}
+NB_AT = Q_RAW_BYTES + 2 * T
+LINE = 64
 
 
 def tile_attend_neu_reglu_topk_kernel(tc, qT, k_words, k_scales, c_words, c_scales, nb, offs, out):
@@ -40,18 +44,16 @@ def tile_attend_neu_reglu_topk_kernel(tc, qT, k_words, k_scales, c_words, c_scal
         offsets = sb.tile([P, N // 16], U16, name="offsets")
         scale_win = []
         for name, src in (("k", k_scales), ("c", c_scales)):
-            win = sb.tile([P, T // 4], I32, name=name + "_scale_win", align_bytes=64)
+            win = shared.tile([P, T // 4], I32, name=name + "_scale_win", align_bytes=64, offset=WIN_AT[name])
             nc.vector.memset(win[:ROW0, :], 0)
             nc.sync.dma_start(win[ROW0:, :], src.bitcast(I32).rearrange("o f t -> (o f) t"))
             scale_win.append(win)
             if name == "k":
                 nc.sync.dma_start(offsets[:], offs)
 
-        nb_cols = sb.tile([P, BANKS, BLOCKS], F32, name="nb_cols", tag="q_slot", align_bytes=64)
-        nc.sync.dma_start(nb_cols[:], nb[0].rearrange("(n b j) -> n b j", b=BANKS, j=BLOCKS))
-
-        planes = sb.tile([P, PASSES, 2, N // 4], I32, name="planes", align_bytes=64)
-        nc.vector.memset(planes[:], 0)
+        nb_tile = shared.tile([P, 2, BANKS, BLOCKS], F32, name="nb_tile", align_bytes=64, offset=NB_AT)
+        nb_cols = nb_tile[:, 0]
+        nc.sync.dma_start(nb_cols, nb[0].rearrange("(n b j) -> n b j", b=BANKS, j=BLOCKS))
 
         k_win = sb.tile([P, T], I32, name="k_win", align_bytes=64)
         q_raw = shared.tile([P, PASSES, PACK, NQ], F32, name="q_raw", align_bytes=64, offset=0)
@@ -80,12 +82,16 @@ def tile_attend_neu_reglu_topk_kernel(tc, qT, k_words, k_scales, c_words, c_scal
         picked_scales = sb.tile([P, 2, N], U8, name="picked_scales", align_bytes=64)
         for i in range(2):
             nc.vector.tensor_copy(picked_scales[:, i, :], scale_win[i][:].bitcast(U8).indirect(offsets[:]))
+        planes = [
+            shared.tile([P, (2 * N + LINE) // 4], I32, name="plane0", align_bytes=64, offset=NB_AT - 2 * N),
+            shared.tile([P, 2 * N // 4], I32, name="plane1", align_bytes=64, offset=WIN_AT["c"]),
+        ]
         for o in range(PASSES):
             for quad in range(QUADS):
                 first = ROW0 + 16 * o + 4 * quad
-                queue = nc.gpsimd if (o, quad) == (PASSES - 1, QUADS - 1) else nc.sync
+                queue = nc.scalar if o == 0 else nc.gpsimd if quad == QUADS - 1 else nc.sync
                 queue.dma_start(
-                    planes[QUAD * quad : QUAD * quad + 4, o].rearrange("p i n -> p (i n)"),
+                    planes[o][QUAD * quad : QUAD * quad + 4, : 2 * N // 4],
                     picked_scales[first : first + 4].rearrange("p i n -> p (i n)").bitcast(I32),
                 )
 
@@ -102,7 +108,7 @@ def tile_attend_neu_reglu_topk_kernel(tc, qT, k_words, k_scales, c_words, c_scal
         nb_picked = sb.tile([P, N], F32, name="nb_picked", align_bytes=64)
         nc.vector.tensor_copy(nb_picked[:], nb_win[:].indirect(offsets[:]))
 
-        q_bf = sb.tile([P, PASSES, NQ, PACK], BF16, name="q_bf", tag="q_slot", align_bytes=64)
+        q_bf = shared.tile([P, PASSES, NQ, PACK], BF16, name="q_bf", align_bytes=64, offset=NB_AT + LINE)
         for o in range(PASSES):
             nc.scalar.copy(
                 q_bf[:, o].rearrange("p (c i) j -> p c j i", i=PACK),
@@ -128,7 +134,7 @@ def tile_attend_neu_reglu_topk_kernel(tc, qT, k_words, k_scales, c_words, c_scal
                 )
 
         a = ps.tile([P, N], F32, name="a")
-        product(a[:], lambda o: k_split[:, o, :], lambda o: planes[:, o, 0, :].bitcast(U8), (0, 1))
+        product(a[:], lambda o: k_split[:, o, :], lambda o: planes[o][:].bitcast(U8)[:, :N], (0, 1))
 
         c_pairs = shared.tile([P, PARTS, PART], U32, name="c_pairs", align_bytes=64, offset=0)
         for s in range(PARTS):
@@ -149,7 +155,7 @@ def tile_attend_neu_reglu_topk_kernel(tc, qT, k_words, k_scales, c_words, c_scal
                 product(
                     acc[:, c * P : (c + 1) * P],
                     lambda o: split[:, o, 2 * c * P : 2 * (c + 1) * P],
-                    lambda o: planes[:, o, 1, :].bitcast(U8)[:, first : first + P],
+                    lambda o: planes[o][:].bitcast(U8)[:, N + first : N + first + P],
                     (1, 0),
                 )
             z.append(acc)

@@ -26,12 +26,10 @@ ROW0 = P - QUAD
 PARTS = 2
 PART = N // PARTS
 BANK = 512
-BANKS = T // BANK
 BLOCKS = BANK // P
 Q_RAW_BYTES = PASSES * PACK * NQ * 4
-WIN_AT = {"c": Q_RAW_BYTES, "k": Q_RAW_BYTES + T}
-NB_AT = Q_RAW_BYTES + 2 * T
-LINE = 64
+NB_AT = Q_RAW_BYTES
+WIN_AT = {"c": NB_AT + 4 * T, "k": NB_AT + 5 * T}
 
 
 def tile_attend_neu_reglu_topk_kernel(tc, qT, k_words, k_scales, c_words, c_scales, nb, offs, out):
@@ -51,45 +49,36 @@ def tile_attend_neu_reglu_topk_kernel(tc, qT, k_words, k_scales, c_words, c_scal
             if name == "k":
                 nc.sync.dma_start(offsets[:], offs)
 
-        nb_tile = shared.tile([P, 2, BANKS, BLOCKS], F32, name="nb_tile", align_bytes=64, offset=NB_AT)
-        nb_cols = nb_tile[:, 0]
-        nc.sync.dma_start(nb_cols, nb[0].rearrange("(n b j) -> n b j", b=BANKS, j=BLOCKS))
+        nb_win = shared.tile([P, T], F32, name="nb_win", align_bytes=64, offset=NB_AT)
+        nc.vector.memset(nb_win[: P - 1, :], 0.0)
+        nc.sync.dma_start(nb_win[P - 1 :, :], nb[0:1, :])
 
         k_win = sb.tile([P, T], I32, name="k_win", align_bytes=64)
         q_raw = shared.tile([P, PASSES, PACK, NQ], F32, name="q_raw", align_bytes=64, offset=0)
-        nc.sync.dma_start(k_win[:], k_words[0].rearrange("p t b -> p (t b)").bitcast(I32))
         nc.sync.dma_start(
             q_raw[:].rearrange("p o j w -> p o (j w)"),
             qT[0].rearrange("(o p j) w -> p o (j w)", o=PASSES, j=PACK),
         )
+        nc.sync.dma_start(k_win[:], k_words[0].rearrange("p t b -> p (t b)").bitcast(I32))
         c_win = sb.tile([P, T], I32, name="c_win", tag="c_slot", align_bytes=64)
         nc.sync.dma_start(c_win[:], c_words[0].rearrange("p t b -> p (t b)").bitcast(I32))
 
         ident = sb.tile([P, P], F32, name="ident")
         make_identity(nc, ident[:])
 
-        nb_win = sb.tile([P, T], F32, name="nb_win", align_bytes=64)
-        for b in range(BANKS):
-            spread = ps.tile([P, BLOCKS, P], F32, name="spread%d" % b)
-            for j in range(BLOCKS):
-                nc.tensor.transpose(spread[:, j, :], nb_cols[:, b, j : j + 1].to_broadcast([P, P]), ident[:])
-            nc.scalar.activation(
-                nb_win[:].rearrange("p (n b j) -> p b n j", b=BANKS, j=BLOCKS)[:, b],
-                spread[:].rearrange("p j n -> p n j"),
-                ACT.Copy,
-            )
-
         picked_scales = sb.tile([P, 2, N], U8, name="picked_scales", align_bytes=64)
         for i in range(2):
             nc.vector.tensor_copy(picked_scales[:, i, :], scale_win[i][:].bitcast(U8).indirect(offsets[:]))
+        nb_picked = sb.tile([P, N], F32, name="nb_picked", align_bytes=64)
+        nc.vector.tensor_copy(nb_picked[:], nb_win[:].indirect(offsets[:]))
         planes = [
-            shared.tile([P, (2 * N + LINE) // 4], I32, name="plane0", align_bytes=64, offset=NB_AT - 2 * N),
+            shared.tile([P, 2 * N // 4], I32, name="plane0", align_bytes=64, offset=WIN_AT["k"]),
             shared.tile([P, 2 * N // 4], I32, name="plane1", align_bytes=64, offset=WIN_AT["c"]),
         ]
         for o in range(PASSES):
             for quad in range(QUADS):
                 first = ROW0 + 16 * o + 4 * quad
-                queue = nc.scalar if o == 0 else nc.gpsimd if quad == QUADS - 1 else nc.sync
+                queue = nc.gpsimd if (o, quad) == (PASSES - 1, QUADS - 1) else nc.sync
                 queue.dma_start(
                     planes[o][QUAD * quad : QUAD * quad + 4, : 2 * N // 4],
                     picked_scales[first : first + 4].rearrange("p i n -> p (i n)").bitcast(I32),
@@ -105,15 +94,25 @@ def tile_attend_neu_reglu_topk_kernel(tc, qT, k_words, k_scales, c_words, c_scal
                 k_split[:, :, 2 * s * PART : 2 * (s + 1) * PART].bitcast(U16),
                 k_pairs[:, s, :].bitcast(U16).rearrange("p (n o) -> p o n", o=PASSES),
             )
-        nb_picked = sb.tile([P, N], F32, name="nb_picked", align_bytes=64)
-        nc.vector.tensor_copy(nb_picked[:], nb_win[:].indirect(offsets[:]))
 
-        q_bf = shared.tile([P, PASSES, NQ, PACK], BF16, name="q_bf", align_bytes=64, offset=NB_AT + LINE)
+        turned = ps.tile([P, BLOCKS, P], F32, name="turned")
+        for j in range(BLOCKS):
+            nc.tensor.transpose(turned[:, j, :], nb_picked[:, j * P : (j + 1) * P], ident[:])
+
+        q_bf = sb.tile([P, PASSES, NQ, PACK], BF16, name="q_bf", align_bytes=64)
         for o in range(PASSES):
             nc.scalar.copy(
                 q_bf[:, o].rearrange("p (c i) j -> p c j i", i=PACK),
                 q_raw[:, o].rearrange("p j (c i) -> p c j i", i=PACK),
             )
+
+        nb_cols = shared.tile([P, BLOCKS], F32, name="nb_cols", align_bytes=64, offset=4 * N)
+        nc.scalar.copy(nb_cols[:], turned[:, :, P - 1])
+        spread = ps.tile([P, BLOCKS, P], F32, name="spread")
+        for j in range(BLOCKS):
+            nc.tensor.transpose(spread[:, j, :], nb_cols[:, j : j + 1].to_broadcast([P, P]), ident[:])
+        nb_rows = sb.tile([P, N], F32, name="nb_rows", align_bytes=64)
+        nc.scalar.copy(nb_rows[:], spread[:].rearrange("p j n -> p (j n)"))
 
         q_codes = sb.tile([P, PASSES * NQ], U32, name="q_codes", align_bytes=64)
         q_scales = sb.tile([P, PASSES * NQ], U8, name="q_scales", align_bytes=64)
@@ -133,7 +132,7 @@ def tile_attend_neu_reglu_topk_kernel(tc, qT, k_words, k_scales, c_words, c_scal
                     stop=(o == order[-1]),
                 )
 
-        a = ps.tile([P, N], F32, name="a")
+        a = ps.tile([P, N], F32, name="a", tag="turned")
         product(a[:], lambda o: k_split[:, o, :], lambda o: planes[o][:].bitcast(U8)[:, :N], (0, 1))
 
         c_pairs = shared.tile([P, PARTS, PART], U32, name="c_pairs", align_bytes=64, offset=0)
@@ -149,23 +148,34 @@ def tile_attend_neu_reglu_topk_kernel(tc, qT, k_words, k_scales, c_words, c_scal
                     split[:, :, 2 * n0 : 2 * (n0 + step)].bitcast(U16),
                     c_pairs[:, s, n0 : n0 + step].bitcast(U16).rearrange("p (n o) -> p o n", o=PASSES),
                 )
-            acc = ps.tile([P, PART], F32, name="z%d" % s)
+            width = PART if s == 0 else P
             for c in range(PART // P):
                 first = s * PART + c * P
+                if c * P % width == 0:
+                    acc = ps.tile([P, width], F32, name="z%d" % first)
+                    z.append((first, width, acc))
                 product(
-                    acc[:, c * P : (c + 1) * P],
+                    acc[:, c * P % width : c * P % width + P],
                     lambda o: split[:, o, 2 * c * P : 2 * (c + 1) * P],
                     lambda o: planes[o][:].bitcast(U8)[:, N + first : N + first + P],
                     (1, 0),
                 )
-            z.append(acc)
 
         gate = sb.tile([P, N], F32, name="gate", tag="c_slot", align_bytes=64)
         for s in range(PARTS):
             cols = slice(s * PART, (s + 1) * PART)
-            nc.vector.tensor_tensor(gate[:, cols], a[:, cols], nb_picked[:, cols], ALU.add)
+            nc.vector.tensor_tensor(gate[:, cols], a[:, cols], nb_rows[:, cols], ALU.add)
         for s in range(PARTS):
             cols = slice(s * PART, (s + 1) * PART)
             result = sb.tile([P, PART], F32, name="result%d" % s)
-            nc.vector.scalar_tensor_tensor(result[:], gate[:, cols], 0.0, z[s][:], ALU.max, ALU.mult)
+            for first, width, acc in z:
+                if first // PART == s:
+                    nc.vector.scalar_tensor_tensor(
+                        result[:, first % PART : first % PART + width],
+                        gate[:, first : first + width],
+                        0.0,
+                        acc[:],
+                        ALU.max,
+                        ALU.mult,
+                    )
             nc.sync.dma_start(out[0, :, cols], result[:])

@@ -22,7 +22,7 @@ PACK = 4
 PASSES = D // (P * PACK)
 QUAD = 32
 QUADS = P // QUAD
-ROW0 = P - QUAD
+ROW0 = QUAD
 PARTS = 2
 PART = N // PARTS
 BANK = 512
@@ -40,25 +40,25 @@ def tile_attend_neu_reglu_topk_kernel(tc, qT, k_words, k_scales, c_words, c_scal
         ps = ctx.enter_context(tc.psum_pool(name="ps", bufs=1))
 
         offsets = sb.tile([P, N // 16], U16, name="offsets")
+        nc.sync.dma_start(offsets[:], offs)
         scale_win = []
-        for name, src in (("k", k_scales), ("c", c_scales)):
+        for name in ("k", "c"):
             win = shared.tile([P, T // 4], I32, name=name + "_scale_win", align_bytes=64, offset=WIN_AT[name])
-            nc.vector.memset(win[:ROW0, :], 0)
-            nc.sync.dma_start(win[ROW0:, :], src.bitcast(I32).rearrange("o f t -> (o f) t"))
+            nc.vector.memset(win[:], 0)
             scale_win.append(win)
-            if name == "k":
-                nc.sync.dma_start(offsets[:], offs)
 
         nb_win = shared.tile([P, T], F32, name="nb_win", align_bytes=64, offset=NB_AT)
         nc.vector.memset(nb_win[: P - 1, :], 0.0)
         nc.sync.dma_start(nb_win[P - 1 :, :], nb[0:1, :])
 
-        k_win = sb.tile([P, T], I32, name="k_win", align_bytes=64)
         q_raw = shared.tile([P, PASSES, PACK, NQ], F32, name="q_raw", align_bytes=64, offset=0)
         nc.sync.dma_start(
             q_raw[:].rearrange("p o j w -> p o (j w)"),
             qT[0].rearrange("(o p j) w -> p o (j w)", o=PASSES, j=PACK),
         )
+        for win, src in zip(scale_win, (k_scales, c_scales)):
+            nc.sync.dma_start(win[ROW0 : ROW0 + 2 * QUAD : 2, :], src.bitcast(I32).rearrange("o f t -> f o t"))
+        k_win = sb.tile([P, T], I32, name="k_win", align_bytes=64)
         nc.sync.dma_start(k_win[:], k_words[0].rearrange("p t b -> p (t b)").bitcast(I32))
         c_win = sb.tile([P, T], I32, name="c_win", tag="c_slot", align_bytes=64)
         nc.sync.dma_start(c_win[:], c_words[0].rearrange("p t b -> p (t b)").bitcast(I32))
@@ -66,23 +66,20 @@ def tile_attend_neu_reglu_topk_kernel(tc, qT, k_words, k_scales, c_words, c_scal
         ident = sb.tile([P, P], F32, name="ident")
         make_identity(nc, ident[:])
 
+        nb_picked = sb.tile([P, N], F32, name="nb_picked", align_bytes=64)
+        nc.vector.tensor_copy(nb_picked[:], nb_win[:].indirect(offsets[:]))
         picked_scales = sb.tile([P, 2, N], U8, name="picked_scales", align_bytes=64)
         for i in range(2):
             nc.vector.tensor_copy(picked_scales[:, i, :], scale_win[i][:].bitcast(U8).indirect(offsets[:]))
-        nb_picked = sb.tile([P, N], F32, name="nb_picked", align_bytes=64)
-        nc.vector.tensor_copy(nb_picked[:], nb_win[:].indirect(offsets[:]))
-        planes = [
-            shared.tile([P, 2 * N // 4], I32, name="plane0", align_bytes=64, offset=WIN_AT["k"]),
-            shared.tile([P, 2 * N // 4], I32, name="plane1", align_bytes=64, offset=WIN_AT["c"]),
-        ]
-        for o in range(PASSES):
-            for quad in range(QUADS):
-                first = ROW0 + 16 * o + 4 * quad
-                queue = nc.gpsimd if (o, quad) == (PASSES - 1, QUADS - 1) else nc.sync
-                queue.dma_start(
-                    planes[o][QUAD * quad : QUAD * quad + 4, : 2 * N // 4],
-                    picked_scales[first : first + 4].rearrange("p i n -> p (i n)").bitcast(I32),
-                )
+        plane = shared.tile([P, PASSES, 2, N // 4], I32, name="plane", align_bytes=64, offset=WIN_AT["k"])
+        last = QUADS - 1
+        moves = [(quad, 0, 1) for quad in range(last)] + [(last, 0, 2)] + [(quad, 1, 2) for quad in range(last)]
+        for quad, i0, i1 in moves:
+            first = ROW0 + 16 * quad
+            nc.sync.dma_start(
+                plane[QUAD * quad : QUAD * quad + 4, :, i0:i1, :].rearrange("p o i n -> p o (i n)"),
+                picked_scales[first : first + 16 : 2, i0:i1, :].rearrange("p i n -> p (i n)").bitcast(I32),
+            )
 
         k_pairs = sb.tile([P, PARTS, PART], U32, name="k_pairs", align_bytes=64)
         for s in range(PARTS):
@@ -133,7 +130,7 @@ def tile_attend_neu_reglu_topk_kernel(tc, qT, k_words, k_scales, c_words, c_scal
                 )
 
         a = ps.tile([P, N], F32, name="a", tag="turned")
-        product(a[:], lambda o: k_split[:, o, :], lambda o: planes[o][:].bitcast(U8)[:, :N], (0, 1))
+        product(a[:], lambda o: k_split[:, o, :], lambda o: plane[:, o, 0, :].bitcast(U8), (0, 1))
 
         c_pairs = shared.tile([P, PARTS, PART], U32, name="c_pairs", align_bytes=64, offset=0)
         for s in range(PARTS):
@@ -157,7 +154,7 @@ def tile_attend_neu_reglu_topk_kernel(tc, qT, k_words, k_scales, c_words, c_scal
                 product(
                     acc[:, c * P % width : c * P % width + P],
                     lambda o: split[:, o, 2 * c * P : 2 * (c + 1) * P],
-                    lambda o: planes[o][:].bitcast(U8)[:, N + first : N + first + P],
+                    lambda o: plane[:, o, 1, :].bitcast(U8)[:, first : first + P],
                     (1, 0),
                 )
 

@@ -66,8 +66,6 @@ def tile_attend_neu_reglu_topk_kernel(tc, qT, k_words, k_scales, c_words, c_scal
         ident = sb.tile([P, P], F32, name="ident")
         make_identity(nc, ident[:])
 
-        nb_picked = sb.tile([P, N], F32, name="nb_picked", align_bytes=64)
-        nc.vector.tensor_copy(nb_picked[:], nb_win[:].indirect(offsets[:]))
         picked_scales = sb.tile([P, 2, N], U8, name="picked_scales", align_bytes=64)
         for i in range(2):
             nc.vector.tensor_copy(picked_scales[:, i, :], scale_win[i][:].bitcast(U8).indirect(offsets[:]))
@@ -92,10 +90,6 @@ def tile_attend_neu_reglu_topk_kernel(tc, qT, k_words, k_scales, c_words, c_scal
                 k_pairs[:, s, :].bitcast(U16).rearrange("p (n o) -> p o n", o=PASSES),
             )
 
-        turned = ps.tile([P, BLOCKS, P], F32, name="turned")
-        for j in range(BLOCKS):
-            nc.tensor.transpose(turned[:, j, :], nb_picked[:, j * P : (j + 1) * P], ident[:])
-
         q_bf = sb.tile([P, PASSES, NQ, PACK], BF16, name="q_bf", align_bytes=64)
         for o in range(PASSES):
             nc.scalar.copy(
@@ -103,6 +97,11 @@ def tile_attend_neu_reglu_topk_kernel(tc, qT, k_words, k_scales, c_words, c_scal
                 q_raw[:, o].rearrange("p j (c i) -> p c j i", i=PACK),
             )
 
+        nb_picked = shared.tile([P, N], F32, name="nb_picked", align_bytes=64, offset=0)
+        nc.scalar.activation(nb_picked[:], nb_win[:].indirect(offsets[:]), ACT.Copy)
+        turned = ps.tile([P, BLOCKS, P], F32, name="turned")
+        for j in range(BLOCKS):
+            nc.tensor.transpose(turned[:, j, :], nb_picked[:, j * P : (j + 1) * P], ident[:])
         nb_cols = shared.tile([P, BLOCKS], F32, name="nb_cols", align_bytes=64, offset=4 * N)
         nc.scalar.copy(nb_cols[:], turned[:, :, P - 1])
         spread = ps.tile([P, BLOCKS, P], F32, name="spread")

@@ -1,7 +1,6 @@
 from contextlib import ExitStack
 
 import concourse.mybir as mybir
-from concourse.masks import make_identity
 
 NQ, D, T, N = 128, 1024, 2048, 512
 FLOPS = 2 * 2 * NQ * D * N
@@ -64,7 +63,17 @@ def tile_attend_neu_reglu_topk_kernel(tc, qT, k_words, k_scales, c_words, c_scal
         nc.sync.dma_start(c_win[:], c_words[0].rearrange("p t b -> p (t b)").bitcast(I32))
 
         ident = sb.tile([P, P], F32, name="ident")
-        make_identity(nc, ident[:])
+        apart = sb.tile([P, P], F32, name="apart")
+        nc.gpsimd.iota(apart[:], [[-1, P]], base=0, channel_multiplier=1, allow_small_or_imprecise_dtypes=True)
+        distance = sb.tile([P, P], F32, name="distance", tag="nb_slot", align_bytes=64)
+        nc.scalar.activation(distance[:], apart[:], ACT.Abs)
+        nc.scalar.activation(ident[:], distance[:], ACT.Relu, bias=1.0, scale=-1.0)
+
+        nb_picked = sb.tile([P, N], F32, name="nb_picked", tag="nb_slot", align_bytes=64)
+        nc.scalar.activation(nb_picked[:], nb_win[:].indirect(offsets[:]), ACT.Copy)
+        turned = ps.tile([P, BLOCKS, P], F32, name="turned")
+        for j in range(BLOCKS):
+            nc.tensor.transpose(turned[:, j, :], nb_picked[:, j * P : (j + 1) * P], ident[:])
 
         picked_scales = sb.tile([P, 2, N], U8, name="picked_scales", align_bytes=64)
         for i in range(2):
@@ -90,18 +99,13 @@ def tile_attend_neu_reglu_topk_kernel(tc, qT, k_words, k_scales, c_words, c_scal
                 k_pairs[:, s, :].bitcast(U16).rearrange("p (n o) -> p o n", o=PASSES),
             )
 
-        q_bf = sb.tile([P, PASSES, NQ, PACK], BF16, name="q_bf", align_bytes=64)
+        q_bf = shared.tile([P, PASSES, NQ, PACK], BF16, name="q_bf", align_bytes=64, offset=NB_AT)
         for o in range(PASSES):
             nc.scalar.copy(
                 q_bf[:, o].rearrange("p (c i) j -> p c j i", i=PACK),
                 q_raw[:, o].rearrange("p j (c i) -> p c j i", i=PACK),
             )
 
-        nb_picked = shared.tile([P, N], F32, name="nb_picked", align_bytes=64, offset=0)
-        nc.scalar.activation(nb_picked[:], nb_win[:].indirect(offsets[:]), ACT.Copy)
-        turned = ps.tile([P, BLOCKS, P], F32, name="turned")
-        for j in range(BLOCKS):
-            nc.tensor.transpose(turned[:, j, :], nb_picked[:, j * P : (j + 1) * P], ident[:])
         nb_cols = shared.tile([P, BLOCKS], F32, name="nb_cols", align_bytes=64, offset=4 * N)
         nc.scalar.copy(nb_cols[:], turned[:, :, P - 1])
         spread = ps.tile([P, BLOCKS, P], F32, name="spread")

@@ -1,6 +1,7 @@
 from contextlib import ExitStack
 
 import concourse.mybir as mybir
+from concourse.masks import make_identity
 
 NQ, D, T, N = 128, 1024, 2048, 512
 FLOPS = 2 * 2 * NQ * D * N
@@ -27,8 +28,7 @@ PART = N // PARTS
 BANK = 512
 BLOCKS = BANK // P
 Q_RAW_BYTES = PASSES * PACK * NQ * 4
-NB_AT = Q_RAW_BYTES
-WIN_AT = {"c": NB_AT + 4 * T, "k": NB_AT + 5 * T}
+WIN_AT = {"c": Q_RAW_BYTES, "k": Q_RAW_BYTES + T}
 
 
 def tile_attend_neu_reglu_topk_kernel(tc, qT, k_words, k_scales, c_words, c_scales, nb, offs, out):
@@ -38,23 +38,21 @@ def tile_attend_neu_reglu_topk_kernel(tc, qT, k_words, k_scales, c_words, c_scal
         shared = ctx.enter_context(tc.tile_pool(name="shared", bufs=1))
         ps = ctx.enter_context(tc.psum_pool(name="ps", bufs=1))
 
+        q_raw = shared.tile([P, PASSES, PACK, NQ], F32, name="q_raw", align_bytes=64, offset=0)
+        nc.sync.dma_start(
+            q_raw[:].rearrange("p o j w -> p o (j w)"),
+            qT[0].rearrange("(o p j) w -> p o (j w)", o=PASSES, j=PACK),
+        )
         offsets = sb.tile([P, N // 16], U16, name="offsets")
         nc.sync.dma_start(offsets[:], offs)
+        nb_cols = sb.tile([P, T // P], F32, name="nb_cols", align_bytes=64)
+        nc.sync.dma_start(nb_cols[:], nb[0].rearrange("(p j) -> p j", p=P))
         scale_win = []
         for name in ("k", "c"):
             win = shared.tile([P, T // 4], I32, name=name + "_scale_win", align_bytes=64, offset=WIN_AT[name])
             nc.vector.memset(win[:], 0)
             scale_win.append(win)
 
-        nb_win = shared.tile([P, T], F32, name="nb_win", align_bytes=64, offset=NB_AT)
-        nc.vector.memset(nb_win[: P - 1, :], 0.0)
-        nc.sync.dma_start(nb_win[P - 1 :, :], nb[0:1, :])
-
-        q_raw = shared.tile([P, PASSES, PACK, NQ], F32, name="q_raw", align_bytes=64, offset=0)
-        nc.sync.dma_start(
-            q_raw[:].rearrange("p o j w -> p o (j w)"),
-            qT[0].rearrange("(o p j) w -> p o (j w)", o=PASSES, j=PACK),
-        )
         for win, src in zip(scale_win, (k_scales, c_scales)):
             nc.sync.dma_start(win[ROW0 : ROW0 + 2 * QUAD : 2, :], src.bitcast(I32).rearrange("o f t -> f o t"))
         k_win = sb.tile([P, T], I32, name="k_win", align_bytes=64)
@@ -63,17 +61,18 @@ def tile_attend_neu_reglu_topk_kernel(tc, qT, k_words, k_scales, c_words, c_scal
         nc.sync.dma_start(c_win[:], c_words[0].rearrange("p t b -> p (t b)").bitcast(I32))
 
         ident = sb.tile([P, P], F32, name="ident")
-        apart = sb.tile([P, P], F32, name="apart")
-        nc.gpsimd.iota(apart[:], [[-1, P]], base=0, channel_multiplier=1, allow_small_or_imprecise_dtypes=True)
-        distance = sb.tile([P, P], F32, name="distance", tag="nb_slot", align_bytes=64)
-        nc.scalar.activation(distance[:], apart[:], ACT.Abs)
-        nc.scalar.activation(ident[:], distance[:], ACT.Relu, bias=1.0, scale=-1.0)
+        make_identity(nc, ident[:])
 
-        nb_picked = sb.tile([P, N], F32, name="nb_picked", tag="nb_slot", align_bytes=64)
-        nc.scalar.activation(nb_picked[:], nb_win[:].indirect(offsets[:]), ACT.Copy)
-        turned = ps.tile([P, BLOCKS, P], F32, name="turned")
-        for j in range(BLOCKS):
-            nc.tensor.transpose(turned[:, j, :], nb_picked[:, j * P : (j + 1) * P], ident[:])
+        nb_win = sb.tile([P, T], F32, name="nb_win", align_bytes=64)
+        for b in range(T // BANK):
+            spread = ps.tile([P, BLOCKS, P], F32, name="spread%d" % b)
+            for j in range(BLOCKS):
+                col = b * BLOCKS + j
+                nc.tensor.transpose(spread[:, j, :], nb_cols[:, col : col + 1].to_broadcast([P, P]), ident[:])
+            nc.scalar.copy(
+                nb_win[:].rearrange("p (m j) -> p m j", m=P)[:, :, b * BLOCKS : (b + 1) * BLOCKS],
+                spread[:].rearrange("p j m -> p m j"),
+            )
 
         picked_scales = sb.tile([P, 2, N], U8, name="picked_scales", align_bytes=64)
         for i in range(2):
@@ -99,20 +98,15 @@ def tile_attend_neu_reglu_topk_kernel(tc, qT, k_words, k_scales, c_words, c_scal
                 k_pairs[:, s, :].bitcast(U16).rearrange("p (n o) -> p o n", o=PASSES),
             )
 
-        q_bf = shared.tile([P, PASSES, NQ, PACK], BF16, name="q_bf", align_bytes=64, offset=NB_AT)
+        q_bf = sb.tile([P, PASSES, NQ, PACK], BF16, name="q_bf", align_bytes=64)
         for o in range(PASSES):
             nc.scalar.copy(
                 q_bf[:, o].rearrange("p (c i) j -> p c j i", i=PACK),
                 q_raw[:, o].rearrange("p j (c i) -> p c j i", i=PACK),
             )
 
-        nb_cols = shared.tile([P, BLOCKS], F32, name="nb_cols", align_bytes=64, offset=4 * N)
-        nc.scalar.copy(nb_cols[:], turned[:, :, P - 1])
-        spread = ps.tile([P, BLOCKS, P], F32, name="spread")
-        for j in range(BLOCKS):
-            nc.tensor.transpose(spread[:, j, :], nb_cols[:, j : j + 1].to_broadcast([P, P]), ident[:])
         nb_rows = sb.tile([P, N], F32, name="nb_rows", align_bytes=64)
-        nc.scalar.copy(nb_rows[:], spread[:].rearrange("p j n -> p (j n)"))
+        nc.scalar.activation(nb_rows[:], nb_win[:].indirect(offsets[:]), ACT.Copy)
 
         q_codes = sb.tile([P, PASSES * NQ], U32, name="q_codes", align_bytes=64)
         q_scales = sb.tile([P, PASSES * NQ], U8, name="q_scales", align_bytes=64)
@@ -132,8 +126,16 @@ def tile_attend_neu_reglu_topk_kernel(tc, qT, k_words, k_scales, c_words, c_scal
                     stop=(o == order[-1]),
                 )
 
-        a = ps.tile([P, N], F32, name="a", tag="turned")
-        product(a[:], lambda o: k_split[:, o, :], lambda o: plane[:, o, 0, :].bitcast(U8), (0, 1))
+        a = []
+        for s in range(PARTS):
+            acc = ps.tile([P, PART], F32, name="a%d" % s, tag="spread%d" % s)
+            product(
+                acc[:],
+                lambda o: k_split[:, o, 2 * s * PART : 2 * (s + 1) * PART],
+                lambda o: plane[:, o, 0, :].bitcast(U8)[:, s * PART : (s + 1) * PART],
+                (0, 1),
+            )
+            a.append(acc)
 
         c_pairs = shared.tile([P, PARTS, PART], U32, name="c_pairs", align_bytes=64, offset=0)
         for s in range(PARTS):
@@ -164,7 +166,7 @@ def tile_attend_neu_reglu_topk_kernel(tc, qT, k_words, k_scales, c_words, c_scal
         gate = sb.tile([P, N], F32, name="gate", tag="c_slot", align_bytes=64)
         for s in range(PARTS):
             cols = slice(s * PART, (s + 1) * PART)
-            nc.vector.tensor_tensor(gate[:, cols], a[:, cols], nb_rows[:, cols], ALU.add)
+            nc.vector.tensor_tensor(gate[:, cols], a[s][:], nb_rows[:, cols], ALU.add)
         for s in range(PARTS):
             cols = slice(s * PART, (s + 1) * PART)
             result = sb.tile([P, PART], F32, name="result%d" % s)

@@ -38,6 +38,9 @@ def tile_attend_neu_reglu_topk_kernel(tc, qT, k_words, k_scales, c_words, c_scal
         shared = ctx.enter_context(tc.tile_pool(name="shared", bufs=1))
         ps = ctx.enter_context(tc.psum_pool(name="ps", bufs=1))
 
+        nb_runs = sb.tile([P, P], F32, name="nb_runs", tag="early", align_bytes=64)
+        runs = slice(P - T // P, P)
+        nc.sync.dma_start(nb_runs[runs, :], nb[0].rearrange("(j m) -> j m", m=P))
         q_raw = shared.tile([P, PASSES, PACK, NQ], F32, name="q_raw", align_bytes=64, offset=0)
         nc.sync.dma_start(
             q_raw[:].rearrange("p o j w -> p o (j w)"),
@@ -45,13 +48,12 @@ def tile_attend_neu_reglu_topk_kernel(tc, qT, k_words, k_scales, c_words, c_scal
         )
         offsets = sb.tile([P, N // 16], U16, name="offsets")
         nc.sync.dma_start(offsets[:], offs)
-        nb_cols = sb.tile([P, T // P], F32, name="nb_cols", align_bytes=64)
-        nc.sync.dma_start(nb_cols[:], nb[0].rearrange("(p j) -> p j", p=P))
         scale_win = []
         for name in ("k", "c"):
             win = shared.tile([P, T // 4], I32, name=name + "_scale_win", align_bytes=64, offset=WIN_AT[name])
             nc.vector.memset(win[:], 0)
             scale_win.append(win)
+        nc.vector.memset(nb_runs[: runs.start, :], 0.0)
 
         for win, src in zip(scale_win, (k_scales, c_scales)):
             nc.sync.dma_start(win[ROW0 : ROW0 + 2 * QUAD : 2, :], src.bitcast(I32).rearrange("o f t -> f o t"))
@@ -63,16 +65,17 @@ def tile_attend_neu_reglu_topk_kernel(tc, qT, k_words, k_scales, c_words, c_scal
         ident = sb.tile([P, P], F32, name="ident")
         make_identity(nc, ident[:])
 
+        turned = ps.tile([P, P], F32, name="turned", tag="z0")
+        nc.tensor.transpose(turned[:], nb_runs[:], ident[:])
+        nb_cols = sb.tile([P, T // P], F32, name="nb_cols", align_bytes=64)
+        nc.scalar.copy(nb_cols[:], turned[:, runs])
         nb_win = sb.tile([P, T], F32, name="nb_win", align_bytes=64)
         for b in range(T // BANK):
             spread = ps.tile([P, BLOCKS, P], F32, name="spread%d" % b)
             for j in range(BLOCKS):
                 col = b * BLOCKS + j
                 nc.tensor.transpose(spread[:, j, :], nb_cols[:, col : col + 1].to_broadcast([P, P]), ident[:])
-            nc.scalar.copy(
-                nb_win[:].rearrange("p (m j) -> p m j", m=P)[:, :, b * BLOCKS : (b + 1) * BLOCKS],
-                spread[:].rearrange("p j m -> p m j"),
-            )
+            nc.scalar.copy(nb_win[:, b * BANK : (b + 1) * BANK], spread[:].rearrange("p j m -> p (j m)"))
 
         picked_scales = sb.tile([P, 2, N], U8, name="picked_scales", align_bytes=64)
         for i in range(2):
@@ -98,7 +101,7 @@ def tile_attend_neu_reglu_topk_kernel(tc, qT, k_words, k_scales, c_words, c_scal
                 k_pairs[:, s, :].bitcast(U16).rearrange("p (n o) -> p o n", o=PASSES),
             )
 
-        q_bf = sb.tile([P, PASSES, NQ, PACK], BF16, name="q_bf", align_bytes=64)
+        q_bf = sb.tile([P, PASSES, NQ, PACK], BF16, name="q_bf", tag="early", align_bytes=64)
         for o in range(PASSES):
             nc.scalar.copy(
                 q_bf[:, o].rearrange("p (c i) j -> p c j i", i=PACK),
@@ -154,7 +157,7 @@ def tile_attend_neu_reglu_topk_kernel(tc, qT, k_words, k_scales, c_words, c_scal
             for c in range(PART // P):
                 first = s * PART + c * P
                 if c * P % width == 0:
-                    acc = ps.tile([P, width], F32, name="z%d" % first)
+                    acc = ps.tile([P, width], F32, name="z%d" % first, tag="z%d" % first)
                     z.append((first, width, acc))
                 product(
                     acc[:, c * P % width : c * P % width + P],

@@ -63,7 +63,8 @@ def tile_attend_neu_reglu_topk_kernel(tc, qT, k_words, k_scales, c_words, c_scal
         nc.sync.dma_start(c_win[:], c_words[0].rearrange("p t b -> p (t b)").bitcast(I32))
 
         ident = sb.tile([P, P], F32, name="ident")
-        make_identity(nc, ident[:])
+        nc.vector.memset(ident[:], 0.0)
+        make_identity(nc, ident[:], nomemset=True)
 
         turned = ps.tile([P, P], F32, name="turned", tag="z0")
         nc.tensor.transpose(turned[:], nb_runs[:], ident[:])

@@ -26,6 +26,7 @@ ROW0 = QUAD
 PARTS = 2
 PART = N // PARTS
 BANK = 512
+AXI = 256
 BLOCKS = BANK // P
 Q_RAW_BYTES = PASSES * PACK * NQ * 4
 WIN_AT = {"c": Q_RAW_BYTES, "k": Q_RAW_BYTES + T}
@@ -38,28 +39,28 @@ def tile_attend_neu_reglu_topk_kernel(tc, qT, k_words, k_scales, c_words, c_scal
         shared = ctx.enter_context(tc.tile_pool(name="shared", bufs=1))
         ps = ctx.enter_context(tc.psum_pool(name="ps", bufs=1))
 
-        nb_runs = sb.tile([P, P], F32, name="nb_runs", tag="early", align_bytes=64)
+        nb_runs = sb.tile([P, P], F32, name="nb_runs", tag="early", align_bytes=AXI)
         runs = slice(P - T // P, P)
         nc.sync.dma_start(nb_runs[runs, :], nb[0].rearrange("(j m) -> j m", m=P))
-        q_raw = shared.tile([P, PASSES, PACK, NQ], F32, name="q_raw", align_bytes=64, offset=0)
+        q_raw = shared.tile([P, PASSES, PACK, NQ], F32, name="q_raw", align_bytes=AXI, offset=0)
         nc.sync.dma_start(
             q_raw[:].rearrange("p o j w -> p o (j w)"),
             qT[0].rearrange("(o p j) w -> p o (j w)", o=PASSES, j=PACK),
         )
-        offsets = sb.tile([P, N // 16], U16, name="offsets")
+        offsets = sb.tile([P, N // 16], U16, name="offsets", align_bytes=AXI)
         nc.sync.dma_start(offsets[:], offs)
         scale_win = []
         for name in ("k", "c"):
-            win = shared.tile([P, T // 4], I32, name=name + "_scale_win", align_bytes=64, offset=WIN_AT[name])
+            win = shared.tile([P, T // 4], I32, name=name + "_scale_win", align_bytes=AXI, offset=WIN_AT[name])
             nc.vector.memset(win[:], 0)
             scale_win.append(win)
         nc.vector.memset(nb_runs[: runs.start, :], 0.0)
 
         for win, src in zip(scale_win, (k_scales, c_scales)):
             nc.sync.dma_start(win[ROW0 : ROW0 + 2 * QUAD : 2, :], src.bitcast(I32).rearrange("o f t -> f o t"))
-        k_win = sb.tile([P, T], I32, name="k_win", align_bytes=64)
+        k_win = sb.tile([P, T], I32, name="k_win", align_bytes=AXI)
         nc.sync.dma_start(k_win[:], k_words[0].rearrange("p t b -> p (t b)").bitcast(I32))
-        c_win = sb.tile([P, T], I32, name="c_win", tag="c_slot", align_bytes=64)
+        c_win = sb.tile([P, T], I32, name="c_win", tag="c_slot", align_bytes=AXI)
         nc.sync.dma_start(c_win[:], c_words[0].rearrange("p t b -> p (t b)").bitcast(I32))
 
         ident = sb.tile([P, P], F32, name="ident")
@@ -68,9 +69,9 @@ def tile_attend_neu_reglu_topk_kernel(tc, qT, k_words, k_scales, c_words, c_scal
 
         turned = ps.tile([P, P], F32, name="turned", tag="z0")
         nc.tensor.transpose(turned[:], nb_runs[:], ident[:])
-        nb_cols = sb.tile([P, T // P], F32, name="nb_cols", align_bytes=64)
+        nb_cols = sb.tile([P, T // P], F32, name="nb_cols", align_bytes=AXI)
         nc.scalar.copy(nb_cols[:], turned[:, runs])
-        nb_win = sb.tile([P, T], F32, name="nb_win", align_bytes=64)
+        nb_win = sb.tile([P, T], F32, name="nb_win", align_bytes=AXI)
         for b in range(T // BANK):
             spread = ps.tile([P, BLOCKS, P], F32, name="spread%d" % b)
             for j in range(BLOCKS):
@@ -78,10 +79,10 @@ def tile_attend_neu_reglu_topk_kernel(tc, qT, k_words, k_scales, c_words, c_scal
                 nc.tensor.transpose(spread[:, j, :], nb_cols[:, col : col + 1].to_broadcast([P, P]), ident[:])
             nc.scalar.copy(nb_win[:, b * BANK : (b + 1) * BANK], spread[:].rearrange("p j m -> p (j m)"))
 
-        picked_scales = sb.tile([P, 2, N], U8, name="picked_scales", align_bytes=64)
+        picked_scales = sb.tile([P, 2, N], U8, name="picked_scales", align_bytes=AXI)
         for i in range(2):
             nc.vector.tensor_copy(picked_scales[:, i, :], scale_win[i][:].bitcast(U8).indirect(offsets[:]))
-        plane = shared.tile([P, PASSES, 2, N // 4], I32, name="plane", align_bytes=64, offset=WIN_AT["k"])
+        plane = shared.tile([P, PASSES, 2, N // 4], I32, name="plane", align_bytes=AXI, offset=WIN_AT["k"])
         last = QUADS - 1
         moves = [(quad, 0, 1) for quad in range(last)] + [(last, 0, 2)] + [(quad, 1, 2) for quad in range(last)]
         for quad, i0, i1 in moves:
@@ -91,29 +92,29 @@ def tile_attend_neu_reglu_topk_kernel(tc, qT, k_words, k_scales, c_words, c_scal
                 picked_scales[first : first + 16 : 2, i0:i1, :].rearrange("p i n -> p (i n)").bitcast(I32),
             )
 
-        k_pairs = sb.tile([P, PARTS, PART], U32, name="k_pairs", align_bytes=64)
+        k_pairs = sb.tile([P, PARTS, PART], U32, name="k_pairs", align_bytes=AXI)
         for s in range(PARTS):
             cols = slice(s * PART // 16, (s + 1) * PART // 16)
             nc.vector.tensor_copy(k_pairs[:, s, :], k_win[:].bitcast(U32).indirect(offsets[:, cols]))
-        k_split = sb.tile([P, PASSES, 2 * N], U8, name="k_split", align_bytes=64)
+        k_split = sb.tile([P, PASSES, 2 * N], U8, name="k_split", align_bytes=AXI)
         for s in range(PARTS):
             nc.vector.tensor_copy(
                 k_split[:, :, 2 * s * PART : 2 * (s + 1) * PART].bitcast(U16),
                 k_pairs[:, s, :].bitcast(U16).rearrange("p (n o) -> p o n", o=PASSES),
             )
 
-        q_bf = sb.tile([P, PASSES, NQ, PACK], BF16, name="q_bf", tag="early", align_bytes=64)
+        q_bf = sb.tile([P, PASSES, NQ, PACK], BF16, name="q_bf", tag="early", align_bytes=AXI)
         for o in range(PASSES):
             nc.scalar.copy(
                 q_bf[:, o].rearrange("p (c i) j -> p c j i", i=PACK),
                 q_raw[:, o].rearrange("p j (c i) -> p c j i", i=PACK),
             )
 
-        nb_rows = sb.tile([P, N], F32, name="nb_rows", align_bytes=64)
+        nb_rows = sb.tile([P, N], F32, name="nb_rows", align_bytes=AXI)
         nc.scalar.activation(nb_rows[:], nb_win[:].indirect(offsets[:]), ACT.Copy)
 
-        q_codes = sb.tile([P, PASSES * NQ], U32, name="q_codes", align_bytes=64)
-        q_scales = sb.tile([P, PASSES * NQ], U8, name="q_scales", align_bytes=64)
+        q_codes = sb.tile([P, PASSES * NQ], U32, name="q_codes", align_bytes=AXI)
+        q_scales = sb.tile([P, PASSES * NQ], U8, name="q_scales", align_bytes=AXI)
         nc.vector.quantize_mx(
             out=q_codes[:].bitcast(FP8X4), scales=q_scales[:], in_=q_bf[:].rearrange("p o w j -> p (o w j)")
         )
@@ -141,13 +142,13 @@ def tile_attend_neu_reglu_topk_kernel(tc, qT, k_words, k_scales, c_words, c_scal
             )
             a.append(acc)
 
-        c_pairs = shared.tile([P, PARTS, PART], U32, name="c_pairs", align_bytes=64, offset=0)
+        c_pairs = shared.tile([P, PARTS, PART], U32, name="c_pairs", align_bytes=AXI, offset=0)
         for s in range(PARTS):
             cols = slice(s * PART // 16, (s + 1) * PART // 16)
             nc.vector.tensor_copy(c_pairs[:, s, :], c_win[:].bitcast(U32).indirect(offsets[:, cols]))
         z = []
         for s in range(PARTS):
-            split = sb.tile([P, PASSES, 2 * PART], U8, name="c_split%d" % s, align_bytes=64)
+            split = sb.tile([P, PASSES, 2 * PART], U8, name="c_split%d" % s, align_bytes=AXI)
             step = P if s == 0 else PART
             for n0 in range(0, PART, step):
                 nc.vector.tensor_copy(
@@ -167,13 +168,13 @@ def tile_attend_neu_reglu_topk_kernel(tc, qT, k_words, k_scales, c_words, c_scal
                     (1, 0),
                 )
 
-        gate = sb.tile([P, N], F32, name="gate", tag="c_slot", align_bytes=64)
+        gate = sb.tile([P, N], F32, name="gate", tag="c_slot", align_bytes=AXI)
         for s in range(PARTS):
             cols = slice(s * PART, (s + 1) * PART)
             nc.vector.tensor_tensor(gate[:, cols], a[s][:], nb_rows[:, cols], ALU.add)
         for s in range(PARTS):
             cols = slice(s * PART, (s + 1) * PART)
-            result = sb.tile([P, PART], F32, name="result%d" % s)
+            result = sb.tile([P, PART], F32, name="result%d" % s, align_bytes=AXI)
             for first, width, acc in z:
                 if first // PART == s:
                     nc.vector.scalar_tensor_tensor(

@@ -39,14 +39,14 @@ def tile_attend_neu_reglu_topk_kernel(tc, qT, k_words, k_scales, c_words, c_scal
         shared = ctx.enter_context(tc.tile_pool(name="shared", bufs=1))
         ps = ctx.enter_context(tc.psum_pool(name="ps", bufs=1))
 
-        nb_runs = sb.tile([P, P], F32, name="nb_runs", tag="early", align_bytes=AXI)
-        runs = slice(P - T // P, P)
-        nc.sync.dma_start(nb_runs[runs, :], nb[0].rearrange("(j m) -> j m", m=P))
         q_raw = shared.tile([P, PASSES, PACK, NQ], F32, name="q_raw", align_bytes=AXI, offset=0)
         nc.sync.dma_start(
             q_raw[:].rearrange("p o j w -> p o (j w)"),
             qT[0].rearrange("(o p j) w -> p o (j w)", o=PASSES, j=PACK),
         )
+        nb_runs = sb.tile([P, P], F32, name="nb_runs", tag="early", align_bytes=AXI)
+        runs = slice(P - T // P, P)
+        nc.sync.dma_start(nb_runs[runs, :], nb[0].rearrange("(j m) -> j m", m=P))
         offsets = sb.tile([P, N // 16], U16, name="offsets", align_bytes=AXI)
         nc.sync.dma_start(offsets[:], offs)
         scale_win = []
@@ -111,7 +111,9 @@ def tile_attend_neu_reglu_topk_kernel(tc, qT, k_words, k_scales, c_words, c_scal
             )
 
         nb_rows = sb.tile([P, N], F32, name="nb_rows", align_bytes=AXI)
-        nc.scalar.activation(nb_rows[:], nb_win[:].indirect(offsets[:]), ACT.Copy)
+        for s in range(PARTS):
+            cols = slice(s * PART // 16, (s + 1) * PART // 16)
+            nc.scalar.activation(nb_rows[:, s * PART : (s + 1) * PART], nb_win[:].indirect(offsets[:, cols]), ACT.Copy)
 
         q_codes = sb.tile([P, PASSES * NQ], U32, name="q_codes", align_bytes=AXI)
         q_scales = sb.tile([P, PASSES * NQ], U8, name="q_scales", align_bytes=AXI)
@@ -149,22 +151,18 @@ def tile_attend_neu_reglu_topk_kernel(tc, qT, k_words, k_scales, c_words, c_scal
         z = []
         for s in range(PARTS):
             split = sb.tile([P, PASSES, 2 * PART], U8, name="c_split%d" % s, align_bytes=AXI)
-            step = P if s == 0 else PART
-            for n0 in range(0, PART, step):
-                nc.vector.tensor_copy(
-                    split[:, :, 2 * n0 : 2 * (n0 + step)].bitcast(U16),
-                    c_pairs[:, s, n0 : n0 + step].bitcast(U16).rearrange("p (n o) -> p o n", o=PASSES),
-                )
+            nc.vector.tensor_copy(
+                split[:].bitcast(U16), c_pairs[:, s, :].bitcast(U16).rearrange("p (n o) -> p o n", o=PASSES)
+            )
             width = PART if s == 0 else P
-            for c in range(PART // P):
-                first = s * PART + c * P
-                if c * P % width == 0:
-                    acc = ps.tile([P, width], F32, name="z%d" % first, tag="z%d" % first)
-                    z.append((first, width, acc))
+            for n0 in range(0, PART, width):
+                first = s * PART + n0
+                acc = ps.tile([P, width], F32, name="z%d" % first, tag="z%d" % first)
+                z.append((first, width, acc))
                 product(
-                    acc[:, c * P % width : c * P % width + P],
-                    lambda o: split[:, o, 2 * c * P : 2 * (c + 1) * P],
-                    lambda o: plane[:, o, 1, :].bitcast(U8)[:, first : first + P],
+                    acc[:],
+                    lambda o: split[:, o, 2 * n0 : 2 * (n0 + width)],
+                    lambda o: plane[:, o, 1, :].bitcast(U8)[:, first : first + width],
                     (1, 0),
                 )
 

@@ -44,7 +44,7 @@ def tile_attend_neu_reglu_topk_kernel(tc, qT, k_words, k_scales, c_words, c_scal
             q_raw[:].rearrange("p o j w -> p o (j w)"),
             qT[0].rearrange("(o p j) w -> p o (j w)", o=PASSES, j=PACK),
         )
-        nb_runs = sb.tile([P, P], F32, name="nb_runs", tag="early", align_bytes=AXI)
+        nb_runs = sb.tile([P, P], F32, name="nb_runs", align_bytes=AXI)
         runs = slice(P - T // P, P)
         nc.sync.dma_start(nb_runs[runs, :], nb[0].rearrange("(j m) -> j m", m=P))
         offsets = sb.tile([P, N // 16], U16, name="offsets", align_bytes=AXI)
@@ -82,16 +82,6 @@ def tile_attend_neu_reglu_topk_kernel(tc, qT, k_words, k_scales, c_words, c_scal
         picked_scales = sb.tile([P, 2, N], U8, name="picked_scales", align_bytes=AXI)
         for i in range(2):
             nc.vector.tensor_copy(picked_scales[:, i, :], scale_win[i][:].bitcast(U8).indirect(offsets[:]))
-        plane = shared.tile([P, PASSES, 2, N // 4], I32, name="plane", align_bytes=AXI, offset=WIN_AT["k"])
-        last = QUADS - 1
-        moves = [(quad, 0, 1) for quad in range(last)] + [(last, 0, 2)] + [(quad, 1, 2) for quad in range(last)]
-        for quad, i0, i1 in moves:
-            first = ROW0 + 16 * quad
-            nc.sync.dma_start(
-                plane[QUAD * quad : QUAD * quad + 4, :, i0:i1, :].rearrange("p o i n -> p o (i n)"),
-                picked_scales[first : first + 16 : 2, i0:i1, :].rearrange("p i n -> p (i n)").bitcast(I32),
-            )
-
         k_pairs = sb.tile([P, PARTS, PART], U32, name="k_pairs", align_bytes=AXI)
         for s in range(PARTS):
             cols = slice(s * PART // 16, (s + 1) * PART // 16)
@@ -103,11 +93,22 @@ def tile_attend_neu_reglu_topk_kernel(tc, qT, k_words, k_scales, c_words, c_scal
                 k_pairs[:, s, :].bitcast(U16).rearrange("p (n o) -> p o n", o=PASSES),
             )
 
-        q_bf = sb.tile([P, PASSES, NQ, PACK], BF16, name="q_bf", tag="early", align_bytes=AXI)
+        q_bf = sb.tile([P, PASSES, NQ, PACK], BF16, name="q_bf", align_bytes=AXI)
         for o in range(PASSES):
             nc.scalar.copy(
                 q_bf[:, o].rearrange("p (c i) j -> p c j i", i=PACK),
                 q_raw[:, o].rearrange("p j (c i) -> p c j i", i=PACK),
+            )
+
+        plane = shared.tile([P, PASSES, 2, N // 4], I32, name="plane", align_bytes=AXI, offset=WIN_AT["k"])
+        last = QUADS - 1
+        moves = [(quad, 0, 1) for quad in range(last)] + [(last, 0, 2)] + [(quad, 1, 2) for quad in range(last)]
+        for quad, i0, i1 in moves:
+            first = ROW0 + 16 * quad
+            queue = nc.scalar if i1 == 1 and quad > 0 else nc.sync
+            queue.dma_start(
+                plane[QUAD * quad : QUAD * quad + 4, :, i0:i1, :].rearrange("p o i n -> p o (i n)"),
+                picked_scales[first : first + 16 : 2, i0:i1, :].rearrange("p i n -> p (i n)").bitcast(I32),
             )
 
         nb_rows = sb.tile([P, N], F32, name="nb_rows", align_bytes=AXI)

@@ -44,7 +44,7 @@ def tile_attend_neu_reglu_topk_kernel(tc, qT, k_words, k_scales, c_words, c_scal
             q_raw[:].rearrange("p o j w -> p o (j w)"),
             qT[0].rearrange("(o p j) w -> p o (j w)", o=PASSES, j=PACK),
         )
-        nb_runs = sb.tile([P, P], F32, name="nb_runs", align_bytes=AXI)
+        nb_runs = sb.tile([P, P], F32, name="nb_runs", tag="early", align_bytes=AXI)
         runs = slice(P - T // P, P)
         nc.sync.dma_start(nb_runs[runs, :], nb[0].rearrange("(j m) -> j m", m=P))
         offsets = sb.tile([P, N // 16], U16, name="offsets", align_bytes=AXI)
@@ -69,8 +69,15 @@ def tile_attend_neu_reglu_topk_kernel(tc, qT, k_words, k_scales, c_words, c_scal
 
         turned = ps.tile([P, P], F32, name="turned", tag="z0")
         nc.tensor.transpose(turned[:], nb_runs[:], ident[:])
-        nb_cols = sb.tile([P, T // P], F32, name="nb_cols", align_bytes=AXI)
+        nb_cols = shared.tile([P, T // P], F32, name="nb_cols", align_bytes=AXI, offset=WIN_AT["k"] + T)
         nc.scalar.copy(nb_cols[:], turned[:, runs])
+        q_bf = sb.tile([P, PASSES, NQ, PACK], BF16, name="q_bf", tag="early", align_bytes=AXI)
+        for o in range(PASSES):
+            nc.scalar.copy(
+                q_bf[:, o].rearrange("p (c i) j -> p c j i", i=PACK),
+                q_raw[:, o].rearrange("p j (c i) -> p c j i", i=PACK),
+            )
+
         nb_win = sb.tile([P, T], F32, name="nb_win", align_bytes=AXI)
         for b in range(T // BANK):
             spread = ps.tile([P, BLOCKS, P], F32, name="spread%d" % b)
@@ -93,14 +100,8 @@ def tile_attend_neu_reglu_topk_kernel(tc, qT, k_words, k_scales, c_words, c_scal
                 k_pairs[:, s, :].bitcast(U16).rearrange("p (n o) -> p o n", o=PASSES),
             )
 
-        q_bf = sb.tile([P, PASSES, NQ, PACK], BF16, name="q_bf", align_bytes=AXI)
-        for o in range(PASSES):
-            nc.scalar.copy(
-                q_bf[:, o].rearrange("p (c i) j -> p c j i", i=PACK),
-                q_raw[:, o].rearrange("p j (c i) -> p c j i", i=PACK),
-            )
-
-        plane = shared.tile([P, PASSES, 2, N // 4], I32, name="plane", align_bytes=AXI, offset=WIN_AT["k"])
+        plane_slot = shared.tile([P, T // 4 + T // P], I32, name="plane_slot", align_bytes=AXI, offset=WIN_AT["k"])
+        plane = plane_slot[:, : T // 4].rearrange("p (o i n) -> p o i n", o=PASSES, i=2)
         last = QUADS - 1
         moves = [(quad, 0, 1) for quad in range(last)] + [(last, 0, 2)] + [(quad, 1, 2) for quad in range(last)]
         for quad, i0, i1 in moves:

from contextlib import ExitStack

import concourse.mybir as mybir
from concourse.masks import make_identity

NQ, D, T, N = 128, 1024, 2048, 512
FLOPS = 2 * 2 * NQ * D * N

F32 = mybir.dt.float32
BF16 = mybir.dt.bfloat16
I32 = mybir.dt.int32
U32 = mybir.dt.uint32
U16 = mybir.dt.uint16
U8 = mybir.dt.uint8
FP8X4 = mybir.dt.float8_e4m3fn_x4
FP4X4 = mybir.dt.float4_e2m1fn_x4
ACT = mybir.ActivationFunctionType
ALU = mybir.AluOpType

P = 128
PACK = 4
PASSES = D // (P * PACK)
QUAD = 32
QUADS = P // QUAD
ROW0 = QUAD
PARTS = 2
PART = N // PARTS
BANK = 512
AXI = 256
BLOCKS = BANK // P
Q_RAW_BYTES = PASSES * PACK * NQ * 4
WIN_AT = {"c": Q_RAW_BYTES, "k": Q_RAW_BYTES + T}


def tile_attend_neu_reglu_topk_kernel(tc, qT, k_words, k_scales, c_words, c_scales, nb, offs, out):
    nc = tc.nc
    with ExitStack() as ctx:
        sb = ctx.enter_context(tc.tile_pool(name="sb", bufs=1))
        shared = ctx.enter_context(tc.tile_pool(name="shared", bufs=1))
        ps = ctx.enter_context(tc.psum_pool(name="ps", bufs=1))

        q_raw = shared.tile([P, PASSES, PACK, NQ], F32, name="q_raw", align_bytes=AXI, offset=0)
        nc.sync.dma_start(
            q_raw[:].rearrange("p o j w -> p o (j w)"),
            qT[0].rearrange("(o p j) w -> p o (j w)", o=PASSES, j=PACK),
        )
        nb_runs = sb.tile([P, P], F32, name="nb_runs", tag="early", align_bytes=AXI)
        runs = slice(P - T // P, P)
        nc.sync.dma_start(nb_runs[runs, :], nb[0].rearrange("(j m) -> j m", m=P))
        offsets = sb.tile([P, N // 16], U16, name="offsets", align_bytes=AXI)
        nc.sync.dma_start(offsets[:], offs)
        scale_win = []
        for name in ("k", "c"):
            win = shared.tile([P, T // 4], I32, name=name + "_scale_win", align_bytes=AXI, offset=WIN_AT[name])
            nc.vector.memset(win[:], 0)
            scale_win.append(win)
        nc.vector.memset(nb_runs[: runs.start, :], 0.0)

        for win, src in zip(scale_win, (k_scales, c_scales)):
            nc.sync.dma_start(win[ROW0 : ROW0 + 2 * QUAD : 2, :], src.bitcast(I32).rearrange("o f t -> f o t"))
        k_win = sb.tile([P, T], I32, name="k_win", align_bytes=AXI)
        nc.sync.dma_start(k_win[:], k_words[0].rearrange("p t b -> p (t b)").bitcast(I32))
        c_win = sb.tile([P, T], I32, name="c_win", tag="c_slot", align_bytes=AXI)
        nc.sync.dma_start(c_win[:], c_words[0].rearrange("p t b -> p (t b)").bitcast(I32))

        ident = sb.tile([P, P], F32, name="ident")
        nc.vector.memset(ident[:], 0.0)
        make_identity(nc, ident[:], nomemset=True)

        turned = ps.tile([P, P], F32, name="turned", tag="z0")
        nc.tensor.transpose(turned[:], nb_runs[:], ident[:])
        nb_cols = shared.tile([P, T // P], F32, name="nb_cols", align_bytes=AXI, offset=WIN_AT["k"] + T)
        nc.scalar.copy(nb_cols[:], turned[:, runs])
        q_bf = sb.tile([P, PASSES, NQ, PACK], BF16, name="q_bf", tag="early", align_bytes=AXI)
        for o in range(PASSES):
            nc.scalar.copy(
                q_bf[:, o].rearrange("p (c i) j -> p c j i", i=PACK),
                q_raw[:, o].rearrange("p j (c i) -> p c j i", i=PACK),
            )

        nb_win = sb.tile([P, T], F32, name="nb_win", align_bytes=AXI)
        for b in range(T // BANK):
            spread = ps.tile([P, BLOCKS, P], F32, name="spread%d" % b)
            for j in range(BLOCKS):
                col = b * BLOCKS + j
                nc.tensor.transpose(spread[:, j, :], nb_cols[:, col : col + 1].to_broadcast([P, P]), ident[:])
            nc.scalar.copy(nb_win[:, b * BANK : (b + 1) * BANK], spread[:].rearrange("p j m -> p (j m)"))

        picked_scales = sb.tile([P, 2, N], U8, name="picked_scales", align_bytes=AXI)
        for i in range(2):
            nc.vector.tensor_copy(picked_scales[:, i, :], scale_win[i][:].bitcast(U8).indirect(offsets[:]))
        k_pairs = sb.tile([P, PARTS, PART], U32, name="k_pairs", align_bytes=AXI)
        for s in range(PARTS):
            cols = slice(s * PART // 16, (s + 1) * PART // 16)
            nc.vector.tensor_copy(k_pairs[:, s, :], k_win[:].bitcast(U32).indirect(offsets[:, cols]))
        k_split = sb.tile([P, PASSES, 2 * N], U8, name="k_split", align_bytes=AXI)
        for s in range(PARTS):
            nc.vector.tensor_copy(
                k_split[:, :, 2 * s * PART : 2 * (s + 1) * PART].bitcast(U16),
                k_pairs[:, s, :].bitcast(U16).rearrange("p (n o) -> p o n", o=PASSES),
            )

        plane_slot = shared.tile([P, T // 4 + T // P], I32, name="plane_slot", align_bytes=AXI, offset=WIN_AT["k"])
        plane = plane_slot[:, : T // 4].rearrange("p (o i n) -> p o i n", o=PASSES, i=2)
        last = QUADS - 1
        moves = [(quad, 0, 1) for quad in range(last)] + [(last, 0, 2)] + [(quad, 1, 2) for quad in range(last)]
        for quad, i0, i1 in moves:
            first = ROW0 + 16 * quad
            queue = nc.scalar if i1 == 1 and quad > 0 else nc.sync
            queue.dma_start(
                plane[QUAD * quad : QUAD * quad + 4, :, i0:i1, :].rearrange("p o i n -> p o (i n)"),
                picked_scales[first : first + 16 : 2, i0:i1, :].rearrange("p i n -> p (i n)").bitcast(I32),
            )

        nb_rows = sb.tile([P, N], F32, name="nb_rows", align_bytes=AXI)
        for s in range(PARTS):
            cols = slice(s * PART // 16, (s + 1) * PART // 16)
            nc.scalar.activation(nb_rows[:, s * PART : (s + 1) * PART], nb_win[:].indirect(offsets[:, cols]), ACT.Copy)

        q_codes = sb.tile([P, PASSES * NQ], U32, name="q_codes", align_bytes=AXI)
        q_scales = sb.tile([P, PASSES * NQ], U8, name="q_scales", align_bytes=AXI)
        nc.vector.quantize_mx(
            out=q_codes[:].bitcast(FP8X4), scales=q_scales[:], in_=q_bf[:].rearrange("p o w j -> p (o w j)")
        )

        def product(acc, words, scales, order):
            for o in order:
                nc.tensor.matmul_mx(
                    out=acc,
                    lhsT=q_codes[:, o * NQ : (o + 1) * NQ].bitcast(FP8X4),
                    lhsT_scale=q_scales[:, o * NQ : (o + 1) * NQ],
                    rhs=words(o).bitcast(FP4X4),
                    rhs_scale=scales(o),
                    start=(o == order[0]),
                    stop=(o == order[-1]),
                )

        a = []
        for s in range(PARTS):
            acc = ps.tile([P, PART], F32, name="a%d" % s, tag="spread%d" % s)
            product(
                acc[:],
                lambda o: k_split[:, o, 2 * s * PART : 2 * (s + 1) * PART],
                lambda o: plane[:, o, 0, :].bitcast(U8)[:, s * PART : (s + 1) * PART],
                (0, 1),
            )
            a.append(acc)

        c_pairs = shared.tile([P, PARTS, PART], U32, name="c_pairs", align_bytes=AXI, offset=0)
        for s in range(PARTS):
            cols = slice(s * PART // 16, (s + 1) * PART // 16)
            nc.vector.tensor_copy(c_pairs[:, s, :], c_win[:].bitcast(U32).indirect(offsets[:, cols]))
        z = []
        for s in range(PARTS):
            split = sb.tile([P, PASSES, 2 * PART], U8, name="c_split%d" % s, align_bytes=AXI)
            nc.vector.tensor_copy(
                split[:].bitcast(U16), c_pairs[:, s, :].bitcast(U16).rearrange("p (n o) -> p o n", o=PASSES)
            )
            width = PART if s == 0 else P
            for n0 in range(0, PART, width):
                first = s * PART + n0
                acc = ps.tile([P, width], F32, name="z%d" % first, tag="z%d" % first)
                z.append((first, width, acc))
                product(
                    acc[:],
                    lambda o: split[:, o, 2 * n0 : 2 * (n0 + width)],
                    lambda o: plane[:, o, 1, :].bitcast(U8)[:, first : first + width],
                    (1, 0),
                )

        gate = sb.tile([P, N], F32, name="gate", tag="c_slot", align_bytes=AXI)
        for s in range(PARTS):
            cols = slice(s * PART, (s + 1) * PART)
            nc.vector.tensor_tensor(gate[:, cols], a[s][:], nb_rows[:, cols], ALU.add)
        for s in range(PARTS):
            cols = slice(s * PART, (s + 1) * PART)
            result = sb.tile([P, PART], F32, name="result%d" % s, align_bytes=AXI)
            for first, width, acc in z:
                if first // PART == s:
                    nc.vector.scalar_tensor_tensor(
                        result[:, first % PART : first % PART + width],
                        gate[:, first : first + width],
                        0.0,
                        acc[:],
                        ALU.max,
                        ALU.mult,
                    )
            nc.sync.dma_start(out[0, :, cols], result[:])
